import numpy as np, ml_dtypes
CORES = [8,136,40,168]
N = 4
BF = ml_dtypes.bfloat16
def gentries(a):
    return np.ascontiguousarray(a.reshape(8, 16, -1).transpose(0, 2, 1)).reshape(8, -1)
def gtable(e):
    e = np.asarray(e); return np.ascontiguousarray(e.reshape(8, -1, 16).transpose(0, 2, 1)).reshape(128, -1).astype(np.int32)
A, W0, B, STEPS, W = 320, 1536, 128, 5, 1920
def tidy(x):
    return np.asarray(x, np.float32).astype(BF).astype(np.float32)
def sign(rng, m, *shape):
    return (m * (2 * rng.integers(0, 2, shape) - 1)).astype(np.float32)
def num(rng, m, *shape):
    return tidy((np.float32(0.25) + np.float32(0.75) * rng.random(shape, dtype=np.float32)) * sign(rng, m, *shape))
def brink(rng, lo, hi, share, *shape):
    e = np.where(rng.random(shape) < 0.5, lo, hi)
    return np.where(rng.random(shape) < share, e, rng.integers(lo, hi + 1, shape))
def parts(rng):
    d = {"ut": num(rng, 0.5, N, 128, W0), "vt": num(rng, 0.5, N, 128, W0), "bs": num(rng, 1.0, N, 128, A)}
    d["zs"] = num(rng, 1.0, N, 128, B); d["cs"] = num(rng, 0.5, N, 128, B); d["tg"] = num(rng, 1.0, N, 128, B)
    d["ui"] = rng.integers(0, W0, (N, 8, 16, A)); d["vo"] = rng.integers(0, W0, (N, 8, 16, A))
    d["ad"] = rng.integers(0, A, (N, 8, B)); d["nx"] = rng.integers(0, A, (N, 8, 2, A))
    hot = np.argsort(rng.random((N, 8, 16)), axis=2)[..., :2]
    for name in ("sl", "tr"):
        w = np.take_along_axis(hot, rng.integers(0, 2, (N, 8, STEPS * B)), 2)
        d[name] = np.where(rng.random(w.shape) < 0.75, w, rng.integers(0, 16, w.shape)).reshape(N, 8, STEPS, B)
    d["hv"] = rng.integers(6, 12, (N, 8, STEPS, B))
    return d
def pack(d):
    out = {}
    for k in ("ut", "vt"): out[k] = d[k].astype(BF)
    for k in ("ui", "vo"): out[k] = np.ascontiguousarray(d[k].reshape(N, 128, A)).astype(np.int32)
    for k in ("bs", "zs", "cs", "tg"): out[k] = d[k].astype(BF)
    out["ad"] = np.stack([gtable(a) for a in d["ad"]])
    for k in ("nx", "sl", "tr", "hv"): out[k] = np.ascontiguousarray(d[k].reshape(N, 8, -1)).astype(np.int32)
    return out
def setup_inputs(rng):
    return pack(parts(rng))
def setup_inputs_spread(rng):
    d = parts(rng)
    for k in ("ut", "vt", "bs", "zs", "cs", "tg"):
        n = d[k].shape[2]
        d[k] = tidy(d[k] * np.repeat(np.exp2(-rng.integers(0, 3, (N, 8, n)).astype(np.float32)), 16, axis=1))
    lo = (W0 * rng.random((N, 8, 16, A)) ** 2).astype(np.int64); hi = W0 - 1 - (W0 * rng.random((N, 8, 16, A)) ** 2).astype(np.int64)
    m = rng.random((N, 8, 1, A)) < rng.random((N, 8, 1, 1))
    d["ui"] = np.where(m, lo, hi); d["vo"] = np.where(m, hi, lo)
    w = rng.random((N, 8, 16, A)) < 0.4
    d["ui"], d["vo"] = np.where(w, d["vo"], d["ui"]), np.where(w, d["ui"], d["vo"])
    d["ad"] = (A * rng.random((N, 8, B)) ** 2).astype(np.int64); d["nx"] = (A * rng.random((N, 8, 2, A)) ** 1.5).astype(np.int64)
    d["sl"] = (16 * rng.random((N, 8, STEPS, B)) ** 2).astype(np.int64); d["tr"] = (16 * rng.random((N, 8, STEPS, B)) ** 2).astype(np.int64)
    d["hv"] = rng.integers(1, 17, (N, 8, STEPS, B))
    return pack(d)
def setup_inputs_ends(rng):
    d = {"ut": sign(rng, 0.5, N, 128, W0), "vt": sign(rng, 0.5, N, 128, W0), "bs": sign(rng, 1.0, N, 128, A)}
    d["zs"] = sign(rng, 1.0, N, 128, B); d["cs"] = sign(rng, 0.5, N, 128, B); d["tg"] = sign(rng, 1.0, N, 128, B)
    d["ui"] = brink(rng, 0, W0 - 1, 0.7, N, 8, 16, A); d["vo"] = brink(rng, 0, W0 - 1, 0.7, N, 8, 16, A)
    for a in (A - 1, 2): d["ui"][..., a] = W0 - 1; d["vo"][..., a] = 0
    for a in (0, A - 3): d["ui"][..., a] = 0; d["vo"][..., a] = W0 - 1
    d["ui"][..., 1] = W0 - 1; d["vo"][..., 1] = W0 - 1
    d["ad"] = brink(rng, 0, A - 1, 0.65, N, 8, B); d["nx"] = brink(rng, 0, A - 1, 0.65, N, 8, 2, A)
    d["ad"][..., B - 1] = A - 1; d["ad"][..., B - 2] = 2; d["ad"][..., 3] = 1; d["ad"][..., 4] = 0; d["ad"][..., 5] = A - 3
    d["sl"] = 15 * rng.integers(0, 2, (N, 8, STEPS, B)); d["tr"] = 15 * rng.integers(0, 2, (N, 8, STEPS, B))
    d["hv"] = brink(rng, 1, 16, 0.8, N, 8, STEPS, B)
    d["hv"][:, :, 0, B - 1] = 16; d["hv"][:, :, 0, B - 2] = 16; d["hv"][:, :, 0, 3:6] = 1
    for p, s in ((127, 1.0), (126, -1.0), (15, 1.0), (14, -1.0)):
        d["ut"][:, p, W0 - 1] = 0.5; d["vt"][:, p, 0] = 0.5 * s; d["zs"][:, p, B - 2:] = 1.0; d["bs"][:, p, A - 1] = s; d["bs"][:, p, 2] = s
    return pack(d)
def setup_inputs_corners(rng):
    d = parts(rng); q = (0, 1, 2, 3, 8, 14, 15, 16); own = np.arange(A)
    for g in range(8):
        same_ad = rng.permutation(np.arange(1, A - 1))[:B]; same_ad[0] = A - 1; same_ad[B - 1] = 0
        k0, k1 = rng.permutation(16)[:2]; kind = g % 4
        for r in range(N):
            n = q[(g + 3 * r) % 8]
            yes = np.argsort(rng.random((16, A)), axis=0) < n
            lo = rng.integers(0, W0 - 1, (16, A)); hi = lo + 1 + (rng.random((16, A)) * (W0 - 1 - lo)).astype(np.int64)
            hi = np.where(rng.random((16, A)) < 0.3, lo + 1, hi); far = rng.random((16, A)) < 0.1
            lo = np.where(far, 0, lo); hi = np.where(far, W0 - 1, hi); tie = rng.random((16, A)) < 0.3
            d["ui"][r, g] = np.where(yes, hi, lo); d["vo"][r, g] = np.where(yes, lo, np.where(tie, lo, hi))
            d["hv"][r, g] = np.clip(n + rng.integers(0, 2, (STEPS, B)), 1, 16)
            if kind == 0:
                d["nx"][r, g, 0] = rng.permutation(A); d["nx"][r, g, 1] = rng.permutation(A)
                d["sl"][r, g] = 15 * rng.integers(0, 2, (STEPS, B)); d["tr"][r, g] = 15 * rng.integers(0, 2, (STEPS, B))
            elif kind == 2:
                d["nx"][r, g] = np.where(rng.random((2, A)) < 0.6, own[None, :], (A - 1) * rng.integers(0, 2, (2, A)))
            else:
                d["ad"][r, g] = same_ad; d["nx"][r, g, 0] = own; d["nx"][r, g, 1] = own if kind == 1 else own[::-1]
                d["sl"][r, g, :2] = k0; d["sl"][r, g, 2:] = k1; d["tr"][r, g] = k0
    return pack(d)
def setup_inputs_crowd(rng):
    d = parts(rng); own = np.arange(A)
    for g in range(8):
        kind = g % 4; p, w = [int(x) for x in rng.permutation(A)[:2]]; k0, k1 = [int(x) for x in rng.permutation(16)[:2]]; ring = rng.permutation(A)[:B]
        if g == 0: p, w = A - 1, 0
        if g == 1: p, w = 0, A - 1
        for r in range(N):
            if kind < 2:
                d["ad"][r, g] = p; d["nx"][r, g] = own[None, :]
                if kind == 1:
                    d["ad"][r, g, B - 1 if g == 1 else 0] = w
                    d["nx"][r, g, 1, p] = w; d["nx"][r, g, 1, w] = p
                d["sl"][r, g] = k0; d["tr"][r, g] = np.where(rng.random((STEPS, B)) < 0.5, k0, k1); d["tr"][r, g, 2] = k0
                if g == 1:
                    yes = (((np.arange(16) - k0) % 16) >= 1) & (((np.arange(16) - k0) % 16) <= 7)
                    for a in (p, w):
                        lo = rng.integers(0, W0 // 2, 16); hi = rng.integers(W0 // 2, W0, 16)
                        d["ui"][r, g, :, a] = np.where(yes, hi, lo); d["vo"][r, g, :, a] = np.where(yes, lo, hi)
                    d["hv"][r, g, :2] = 16; d["hv"][r, g, 0, B - 2] = 1; d["hv"][r, g, 2, B - 2:] = 8
            elif g == 6:
                lo = rng.integers(0, W0 // 2, (16, A)); hi = lo + rng.integers(1, W0 // 2, (16, A)); yes = ((np.arange(16) - k0) % 16)[:, None] < 8
                d["ui"][r, g] = np.where(yes, hi, lo); d["vo"][r, g] = np.where(yes, lo, hi)
                d["ad"][r, g] = ring; d["nx"][r, g, 0] = own; d["nx"][r, g, 0, ring] = np.roll(ring, -1); d["nx"][r, g, 1] = own[::-1]
                d["sl"][r, g] = k0; d["hv"][r, g, :4] = 16; d["hv"][r, g, 4:] = 8
            elif kind == 2:
                d["ad"][r, g] = np.where(rng.random(B) < 0.5, p, w); d["nx"][r, g, 0] = p; d["nx"][r, g, 1] = w
                for a in (p, w):
                    d["ui"][r, g, :8, a] = W0 - 1; d["vo"][r, g, :8, a] = 0; d["ui"][r, g, 8:, a] = 0; d["vo"][r, g, 8:, a] = W0 - 1
                d["hv"][r, g] = 8 + rng.integers(0, 2, (STEPS, B)); d["sl"][r, g] = rng.choice(np.array([0, 8, 15]), (STEPS, B)); d["tr"][r, g] = rng.choice(np.array([0, 8, 15]), (STEPS, B))
            else:
                m0, n0 = [int(x) for x in np.sort(rng.permutation(W0)[:2])]
                if r == 0: m0, n0 = 0, W0 - 1
                if (r + g // 4) % 2: m0, n0 = n0, m0
                d["ui"][r, g] = n0; d["vo"][r, g] = m0
                o = rng.permutation(A)[:B]; d["ad"][r, g] = o; d["nx"][r, g, 0] = rng.permutation(A); d["nx"][r, g, 1] = rng.permutation(A)
                if g == 7: d["ui"][r, g, :, o[0]] = m0; d["vo"][r, g, :, o[0]] = n0
                d["hv"][r, g] = (15 if n0 > m0 else 1) + rng.integers(0, 2, (STEPS, B))
    return pack(d)
def setup_inputs_brim(rng):
    d = parts(rng); one = int(rng.integers(0, 8))
    for r in range(N):
        for g in range(8):
            full = (g == one) == (r % 2 == 0)
            if full and r % 4 < 2:
                d["ad"][r, g] = int(rng.integers(0, A)); continue
            k = int(rng.integers(0, 16)); m = int(rng.integers(0, W0))
            o = d["vo"][r, g]; o[o == m] = (m + 1) % W0; o[k] = m
            d["ad"][r, g] = rng.permutation(A)[:B]
            w = (k + rng.integers(1, 16, B)) % 16
            if full: w[:] = k
            w[B - 1] = k
            d["tr"][r, g, 0] = w
            if not full:
                nm = rng.permutation(W0); nm = nm[nm != m][:B - 1]
                if g == (one + 4) % 8: nm[1] = nm[0]
                o[w[:B - 1], d["ad"][r, g, :B - 1]] = nm
    return pack(d)
def check_ranges(d):
    bad = []
    for k, lo, hi in (("ui", 0, W0 - 1), ("vo", 0, W0 - 1), ("ad", 0, A - 1), ("nx", 0, A - 1), ("sl", 0, 15), ("tr", 0, 15), ("hv", 1, 16)):
        if np.min(d[k]) < lo or np.max(d[k]) > hi: bad.append("range of " + k)
    for k, lo, hi in (("ut", 2.0 ** -5, 0.5), ("vt", 2.0 ** -5, 0.5), ("cs", 2.0 ** -5, 0.5), ("bs", 2.0 ** -4, 1.0), ("zs", 2.0 ** -4, 1.0), ("tg", 2.0 ** -4, 1.0)):
        v = np.abs(np.asarray(d[k]).astype(np.float64))
        if not np.all((v >= lo) & (v <= hi)): bad.append("range of " + k)
    return bad
def first(key, ok):
    w = np.where(ok, key, -1 - np.arange(B)[None, :]); o = np.argsort(w, axis=1, kind="stable"); s = np.take_along_axis(w, o, 1)
    f = np.ones(s.shape, bool); f[:, 1:] = s[:, 1:] != s[:, :-1]
    m = np.zeros(s.shape, bool); np.put_along_axis(m, o, f, 1)
    return m & ok
def name_at(x, k):
    return np.take_along_axis(x, k[:, None, :], 1)[:, 0]
def vector_at(x, k):
    return np.take_along_axis(x, k[:, None, None, :], 2)[:, :, 0]
def moved(x):
    h = B // 2; w = np.roll(x, 1, axis=0); w[..., h:] = np.roll(x, -1, axis=0)[..., h:]
    return w
def reference(ut, vt, ui, vo, bs, zs, cs, tg, ad, nx, sl, tr, hv):
    U = np.zeros((N, 8, 16, W)); V = np.zeros((N, 8, 16, W))
    U[..., :W0] = ut.astype(np.float64).reshape(N, 8, 16, W0); V[..., :W0] = vt.astype(np.float64).reshape(N, 8, 16, W0)
    I = ui.astype(np.int64).reshape(N, 8, 16, A); O = vo.astype(np.int64).reshape(N, 8, 16, A)
    b = bs.astype(np.float64).reshape(N, 8, 16, A); goal = tg.astype(np.float64).reshape(N, 8, 16, B)
    z = zs.astype(np.float64).reshape(N, 8, 16, B); c = cs.astype(np.float64).reshape(N, 8, 16, B)
    a = np.stack([gentries(x) for x in ad]).astype(np.int64); nxt = nx.astype(np.int64)
    sw, tn, hn = [x.astype(np.int64).reshape(N, 8, STEPS, B) for x in (sl, tr, hv)]
    ys = np.zeros((N, 8, 16, STEPS + 1, B))
    for t in range(STEPS + 1):
        zn, cn, an = np.zeros_like(z), np.zeros_like(c), np.zeros_like(a)
        for r in range(N):
            ai = a[r][:, None, :]
            In = np.take_along_axis(I[r], ai, 2); On = np.take_along_axis(O[r], ai, 2)
            pu = np.take_along_axis(U[r], In.reshape(8, 1, 16 * B), 2).reshape(8, 16, 16, B)
            pv = np.take_along_axis(V[r], On.reshape(8, 1, 16 * B), 2).reshape(8, 16, 16, B)
            y = np.take_along_axis(b[r], ai, 2) + 0.0625 * np.add.reduce(pu * pv, axis=2) * z[r]
            ys[r, :, :, t] = y
            if t == STEPS: continue
            e = y - goal[r]
            votes = np.add.reduce((In > On).astype(np.int64), axis=1)
            an[r] = np.take_along_axis(nxt[r], np.where(votes >= hn[r, :, t], A, 0) + a[r], 1)
            zn[r] = np.clip(y, -1.0, 1.0)
            act = first(a[r], np.ones((8, B), bool))
            if t % 2 == 0: X, Y, P, px, py, Pn, Qn = U, V, I, pu, pv, In, On
            else: X, Y, P, px, py, Pn, Qn = V, U, O, pv, pu, On, In
            k, j = sw[r, :, t], tn[r, :, t]
            xk, yk, xj = vector_at(px, k), vector_at(py, k), vector_at(px, j)
            pj, qj = name_at(Pn, j), name_at(Qn, j)
            go = act
            if t >= 2: go = act & (pj < W0 + B * (t // 2 - 1))
            go = first(qj, go)
            n = W0 + B * (t // 2) + np.arange(B)
            cn[r] = np.where(act[:, None, :], xk, c[r])
            more = 0.0625 * (xk - c[r]) * yk; less = 0.0625 * e * xj * z[r]
            for g in range(8):
                s = np.nonzero(act[g])[0]
                X[r, g][:, n[s]] = c[r, g][:, s]
                P[r, g][k[g, s], a[r, g, s]] = n[s]
                b[r, g][:, a[r, g, s]] += more[g][:, s]
                s = np.nonzero(go[g])[0]
                Y[r, g][:, qj[g, s]] -= less[g][:, s]
        if t < STEPS: z, c, a = moved(zn), moved(cn), moved(an)
    return {"ys": ys.reshape(N, 128, (STEPS + 1) * B).astype(np.float32), "fb": b.reshape(N, 128, A).astype(np.float32), "fc": c.reshape(N, 128, B).astype(np.float32)}

def check_inputs(d):
    bad = list(check_ranges(d))
    if not bad:
        for name, y in reference(**d).items():
            for q in range(N):
                v = np.abs(np.asarray(y[q], np.float64)); s = np.sqrt(np.mean(v * v))
                if v.max() > 3 * s or s < 2.0 ** -4: bad.append('%s of rank %d is uneven or too small' % (name, q))
    return bad

@@ -1,0 +1,525 @@
+from concourse.bass import DstId, RemoteDMATransfer
+from concourse.mybir import AluOpType as Alu, ActivationFunctionType as Fn, AxisListType
+
+A, W0, B, STEPS = 320, 1536, 128, 5
+D = 128
+WIDE = W0 + 3 * B
+F, H, HF, I32, U16 = "float32", "bfloat16", "float16", "int32", "uint16"
+
+SB = {
+    "U": (D + WIDE, F), "V": (D + W0 + 2 * B, F), "ub": (W0, H), "vb": (W0, H),
+    "uii": (A, I32), "voi": (A, I32), "NI": (WIDE, F), "NO": (WIDE, F), "base": (WIDE, F),
+    "adi": (8, I32), "nxi": (A, I32), "hqi": (B, I32), "hq": (B, H), "lti": (B, I32), "ltb": (B, H),
+    "zb": (B, H), "tgb": (B, H), "zin": (6 * B, F), "cfin": (B, F), "ain": (6 * 8, F),
+    "J": (A, F), "gq": (B, F), "c80": (80, F), "pci": (8, I32), "col": (16, F), "id16": (16, F), "tmp16": (16, F),
+    "idf": (B, F), "idb": (B, H), "Bb": (B, H), "Bh": (B, HF), "Z": (144, HF), "Z2": (144, H),
+    "half": (B, F), "ones": (B, H), "thr": (B, F), "nthr": (B, H), "irow": (B, H),
+    "iw": (8, F), "ww": (8, F), "wwb": (8, H), "nw": (24, F), "kjf": (80, F), "kj": (80, U16), "lkj": (80, U16),
+    "aw": (6 * 8, U16), "awb": (5 * 8, H), "arep": (5 * B, H), "pq": (6 * 2 * B, F), "off": (6 * 2 * B, U16),
+    "oh": (5 * 2 * B, H), "hn": (5 * B, F), "cmp": (5 * B, H), "rr": (5 * B, H),
+    "wb": (5 * 5 * B, HF), "eq1": (5 * 8 * B, H), "eq2": (5 * 8 * B, H), "qrep": (5 * B, F), "sg": (5 * B, H),
+    "aout": (5 * 8, F), "sm": (5 * 64, F), "tl": (5 * 24, F), "lst": (5 * 24, U16), "lt": (5 * 8, U16),
+    "py": (2 * 2048, F), "prod": (2 * 2048, F), "bg": (6 * B, F), "z16": (6 * B, F), "yo": (6 * B, F),
+    "zout": (5 * B, F), "cout": (5 * B, F), "wo": (10 * B, F), "wide1": (5 * B, H), "hsel": (5 * B, H), "pmx": (80, H), "xz": (5 * B, F),
+    "idn": (B, F), "odd": (B, F), "run": (1024, F), "keep": (512, H), "id1": (B, F), "idnb": (B, H), "sg1": (5 * B, H),
+    "less": (5 * B, F), "more": (5 * B, F),
+}
+PS = ["pS", "pN", "pW", "pR", "pV", "pT", "pY", "pX"]
+SCRATCH = {k: ("sbuf", [128, v[0]], v[1]) for k, v in SB.items()}
+SCRATCH.update({k: ("psum", [128, 512], F) for k in PS})
+DMAS = ["d_ad", "d_ui", "d_vo", "d_ub", "d_vb", "d_zt", "d_nx", "d_h", "d_lt", "d_U", "d_V", "d_c", "d_b", "d_out"]
+SEMAPHORES = (["e_v", "e_s", "e_t", "e_g", "sent"] + DMAS
+              + ["r_%s%d" % (k, t) for k in "azc" for t in range(1, STEPS + 1)])
+
+CY, PE, GATH, SCAT, HOP, WAKE = 1.0, 0.5, 1.6, 3.8, 2500.0, 120.0
+NS, SUMS = [4, 2, 2, 2, 2, 2], ["FFFF", "HHHH", "HHHH", "HHHH", "FFFF", "FFFS"]
+OPT_E, OPT_F, OPT_H = (), (0, 1, 2, 3), False
+ROUNDS, JOG, SLACK, PIECE = 12000, 5000.0, 20, 1000.0
+
+
+def R(name, lo, n, step=1, p=None):
+    return (name, lo, n, step, p)
+
+
+def X(win, off):
+    return ("*", win, off)
+
+
+def plan():
+    ops = []
+
+    def regs(x):
+        if isinstance(x, tuple):
+            if x[0] == "*":
+                return regs(x[1]) + regs(x[2])
+            return [(x[0], x[1], x[1] + (x[2] - 1) * x[3] + 1)]
+        return []
+
+    def add(eng, calls, cost, outs, ins, lat=0.0, sem=None):
+        rd, wr = [], []
+        for o in outs:
+            if o[0] == "*":
+                wr += regs(o[1]); rd += regs(o[2])
+            else:
+                wr += regs(o)
+        for i in ins:
+            rd += regs(i)
+        ops.append({"eng": eng, "calls": calls, "cost": cost, "rd": rd, "wr": wr, "lat": lat, "sem": sem})
+        return len(ops) - 1
+
+    def size(x):
+        return 16 * x[2][2] if x[0] == "*" else x[2]
+
+    def two(x):
+        return x[0] in SB and SB[x[0]][1] in (H, HF, U16)
+
+    def vcost(out, ins, both):
+        n = size(out)
+        if out[0] == "*":
+            return 50 + SCAT * n * CY
+        if ins[0][0] == "*":
+            return 50 + GATH * n * CY
+        if both:
+            k = 1.0 if ins[0][0] in PS or ins[1][0] in PS else 2.0
+        else:
+            k = 0.5 if two(out) and all(two(i) for i in ins) else 1.0
+        return max(64.0, k * n) * CY
+
+    def tt(out, a, b, op):
+        add("v", [("tt", out, a, b, op)], vcost(out, [a, b], True), [out], [a, b])
+
+    def ts(out, a, s1, op0, s2=None, op1=None):
+        add("v", [("ts", out, a, s1, s2, op0, op1)], vcost(out, [a], False), [out], [a, s1, s2])
+
+    def cp(out, a):
+        add("v", [("cp", out, a)], vcost(out, [a], False), [out], [a])
+
+    def ms(out, c):
+        add("v", [("ms", out, c)], max(64.0, size(out) * (0.5 if two(out) else 1.0)), [out], [])
+
+    def act(out, a, fn=Fn.Identity, bias=0.0, scale=1.0):
+        c = 65 + size(out) * CY * (GATH if a[0] == "*" else 1.0)
+        add("s", [("act", out, a, fn, bias, scale)], c, [out], [a, bias, scale])
+
+    def mm(group):
+        c, calls, part, last, gid = 0.0, [], [], None, len(ops)
+        for i, (o, l, r) in enumerate(group):
+            c += max(64, r[2]) * PE * (4 if SB[r[0]][1] == F else 1)
+            calls.append(("mm", o, l, r, i == 0, i == len(group) - 1))
+            part.append((o, l, r))
+            if c >= PIECE * PE or i == len(group) - 1:
+                j = add("t", calls, c, [x[0] for x in part], [x[1] for x in part] + [x[2] for x in part], lat=60.0)
+                ops[j]["grp"], ops[j]["behind"], last = gid, last, j
+                c, calls, part = 0.0, [], []
+
+    def dma(eng, sem, pairs, outs, ins, ns):
+        add(eng, [("dma", o, i, sem) for o, i in pairs], (900.0 if eng == "g" else 80.0) * len(pairs), outs, ins, lat=1800.0 + ns, sem=(sem, 16 * len(pairs)))
+
+    def iota(out, pat, cm=0):
+        add("g", [("iota", out, pat, cm)], 130 + 2 * size(out), [out], [])
+
+    def send(src, dst, sem):
+        s = add("g", [("send", src, dst, sem)], 500.0, [], [src])
+        r = add(None, [], 0.0, [dst], [], lat=HOP, sem=(sem, None))
+        ops[r]["after"] = s
+
+    def In(name, *ix):
+        return ("@", name, ix)
+
+    al = slice(None)
+    dma("y", "d_ad", [(R("adi", 0, 8), In("ad", al, al))], [R("adi", 0, 8)], [], 0)
+    dma("y", "d_vo", [(R("voi", 0, A), In("vo", al, al))], [R("voi", 0, A)], [], 100)
+    dma("s", "d_vb", [(R("vb", 0, W0), In("vt", al, al))], [R("vb", 0, W0)], [], 600)
+    dma("s", "d_ui", [(R("uii", 0, A), In("ui", al, al))], [R("uii", 0, A)], [], 300)
+    dma("y", "d_ub", [(R("ub", 0, W0), In("ut", al, al))], [R("ub", 0, W0)], [], 1000)
+    p80, p40, p1 = slice(0, 80), slice(0, 40), slice(0, 1)
+    ms(R("nxi", 0, A), 0)
+    dma("y", "d_nx", [(R("nxi", 0, A, 1, slice(q, 128, 16)), In("nx", al, slice(q * A, q * A + A))) for q in range(2)], [R("nxi", 0, A)], [], 300)
+    dma("y", "d_h", [(R("hqi", 0, B, 1, p40), In("hv", al, al))], [R("hqi", 0, B)], [], 100)
+    dma("s", "d_zt", [(R("zb", 0, B), In("zs", al, al)), (R("tgb", 0, B), In("tg", al, al))], [R("zb", 0, B), R("tgb", 0, B)], [], 100)
+    dma("y", "d_lt", [(R("lti", 16 * g, 16, 1, slice(40 * q, 40 * q + 40)), In(nm, g, al)) for q, nm in enumerate(("sl", "tr")) for g in range(8)],
+        [R("lti", 0, B)], [], 100)
+    iota(R("pci", 0, 1), [[1, 1]], 1)
+    iota(R("J", 0, B), [[1, B]])
+    iota(R("gq", 0, B), [[1, 8], [0, 16]])
+    act(R("J", B, B), R("J", 0, B), bias=float(B))
+    act(R("J", 2 * B, A - 2 * B), R("J", 0, A - 2 * B), bias=2.0 * B)
+    iota(R("c80", 0, 80), [[0, 10], [256, 8]])
+    ms(R("wide1", 0, 5 * B), 1.0)
+    add("g", [("sel", R("hsel", 0, 5 * B, 1, p40), R("wide1", 0, 5 * B, 1, p40), [[1, 5], [5, 8], [0, 16]], Alu.is_equal, -1)], 170 + 10 * B, [R("hsel", 0, 5 * B)], [R("wide1", 0, 5 * B)])
+    add("g", [("sel", R("pmx", 0, 80, 1, p80), R("wide1", 0, 80, 1, p80), [[8, 5], [40, 2], [1, 8]], Alu.is_equal, -1)], 170 + 160, [R("pmx", 0, 80)], [R("wide1", 0, 80)])
+    if "S" in "".join(SUMS):
+        add("g", [("sel", R("keep", 0, 512), R("wide1", 0, 512), [[0, 32], [1, 16]], Alu.is_gt, 0)], 170 + 1024, [R("keep", 0, 512)], [R("wide1", 0, 512)])
+    dma("g", "d_b", [(R("base", 0, A), In("bs", al, al))], [R("base", 0, A)], [], 300)
+    dma("g", "d_U", [(R("U", D, W0), In("ut", al, al))], [R("U", D, W0)], [], 1500)
+    dma("g", "d_c", [(R("U", D + W0, B), In("cs", al, al))], [R("U", D + W0, B)], [], 200)
+    dma("g", "d_V", [(R("V", D, W0), In("vt", al, al))], [R("V", D, W0)], [], 1500)
+    pc, rc, gc_, r16, sc, bc, vc = [R("col", i, 1) for i in range(7)]
+    ts(R("pci", 1, 1), R("pci", 0, 1), 15, Alu.bitwise_and)
+    ts(R("pci", 2, 1), R("pci", 0, 1), 4, Alu.arith_shift_right)
+    cp(R("col", 0, 3), R("pci", 0, 3))
+    ts(R("idf", 0, B), R("J", 0, B), pc, Alu.is_equal, 1.0 / 16, Alu.mult)
+    act(R("idn", 0, B), R("idf", 0, B), scale=-1.0)
+    act(R("id1", 0, B), R("idf", 0, B), scale=16.0)
+    act(R("idb", 0, B), R("idf", 0, B), scale=16.0)
+    if OPT_F:
+        act(R("idnb", 0, B), R("idf", 0, B), scale=-1.0)
+    ts(R("id16", 0, 16), R("J", 0, 16), rc, Alu.is_equal)
+    ts(R("Bb", 0, B), R("gq", 0, B), gc_, Alu.is_equal)
+    ts(R("Bh", 0, B), R("gq", 0, B), gc_, Alu.is_equal)
+    ms(R("Z2", 0, 144), 0.0)
+    cp(R("Z", 0, 144), R("Z2", 0, 144))
+    ts(R("Z", 15, 8, 16), R("gq", 0, 8, 16), gc_, Alu.is_equal)
+    ts(R("Z2", 15, 8, 16), R("gq", 0, 8, 16), gc_, Alu.is_equal, -128.0, Alu.mult)
+    ms(R("half", 0, B), 0.5); ms(R("ones", 0, B), 1.0)
+    add("v", [("scan", R("thr", 0, B), R("half", 0, B), R("ones", 0, B), 2.5 * 2.0 ** 64, Alu.mult)], 128.0, [R("thr", 0, B)], [R("half", 0, B), R("ones", 0, B)])
+    act(R("nthr", 0, B), R("thr", 0, B), scale=-1.0)
+    act(R("irow", 0, B), R("J", 0, B), scale=1.0 / 2048)
+    act(r16, rc, scale=16.0)
+    act(sc, R("id16", 0, 1), scale=-2048.0, bias=1024.0)
+    act(bc, sc, scale=17.0 if OPT_H else 0.5)
+    ts(R("iw", 0, 8), R("J", 0, 8, 16), rc, Alu.add)
+    tt(R("tmp16", 0, 16), R("thr", 0, 16), R("id16", 0, 16), Alu.mult)
+    add("v", [("red", vc, R("tmp16", 0, 16))], 64.0, [vc], [R("tmp16", 0, 16)])
+    ts(R("ww", 0, 8), R("thr", 0, 8, 16), 1.0 / (6.25 * 2.0 ** 63), Alu.mult, vc, Alu.mult)
+    act(R("wwb", 0, 8), R("ww", 0, 8))
+    for m in range(3):
+        act(R("nw", 8 * m, 8), R("iw", 0, 8), scale=-1.0, bias=-float(W0 + B * m))
+    ts(R("hq", 0, B, 1, p40), R("hqi", 0, B, 1, p40), -2.0 if OPT_H else -1.0, Alu.mult)
+    cp(R("ltb", 0, B, 1, p80), R("lti", 0, B, 1, p80))
+    mm([(R("pR", 0, 80), R("ltb", 0, B, 1, p80), R("pmx", 0, 80, 1, p80))])
+    cp(R("kj", 0, 80), R("pR", 0, 80))
+    tt(R("kjf", 0, 80), R("pR", 0, 80), R("c80", 0, 80), Alu.add)
+    ts(R("lkj", 0, 80), R("kjf", 0, 80), r16, Alu.add)
+    cp(R("aw", 0, 8), R("adi", 0, 8))
+    cp(R("ain", 0, 8), R("adi", 0, 8))
+    cp(R("NO", 0, A), R("voi", 0, A))
+    cp(R("NI", 0, A), R("uii", 0, A))
+
+    for t in range(STEPS + 1):
+        ev = t % 2 == 0
+        n0 = W0 + B * (t // 2)
+        lim = {"U": W0 + B * ((t + 1) // 2), "V": W0 + B * (t // 2)}
+        Xn, Yn, Pn = ("U", "V", "NI") if ev else ("V", "U", "NO")
+        po, qo = (0, B) if ev else (B, 0)
+        aw, af = R("aw", 8 * t, 8), R("ain", 8 * t, 8)
+        pq, off = 2 * B * t, 2 * B * t
+        if t > 0:
+            cp(aw, af)
+        act(R("pq", pq, B), X(R("NI", 0, A), aw))
+        act(R("pq", pq + B, B), X(R("NO", 0, A), aw))
+        cp(R("off", off + qo, B), R("pq", pq + qo, B))
+        cp(R("off", off + po, B), R("pq", pq + po, B))
+        if t < STEPS:
+            wb, sm, tl = 5 * B * t, 64 * t, 24 * t
+            ohk, ohj = R("oh", 2 * B * t, B), R("oh", 2 * B * t + B, B)
+            act(R("pN", 0, 2 * B), R("pq", pq, 2 * B))
+            act(R("oh", 2 * B * t, 2 * B), X(R("id16", 0, 16), R("kj", 16 * t, 16)))
+            act(R("arep", B * t, B), X(R("J", 0, A), aw), bias=-160.0)
+            act(R("awb", 8 * t, 8), af, bias=-160.0)
+            mm([(R("pR", B, B), R("idb", 0, B), ohk), (R("pR", B, B), R("ones", 0, B, 1, p1), R("irow", 0, B, 1, p1))])
+            act(R("hn", B * t, B), R("pR", B, B), scale=2048.0, bias=n0 - 2048.0)
+            if OPT_H:
+                mm([(R("pV", 2 * B, B), R("idf", 0, B), R("pq", pq, B)), (R("pV", 2 * B, B), R("idn", 0, B), R("pq", pq + B, B))])
+                act(R("cmp", B * t, B), R("pV", 2 * B, B), Fn.Sign, bias=-1.0 / 32)
+            else:
+                tt(R("cmp", B * t, B), R("pN", 0, B), R("pq", pq + B, B), Alu.is_gt)
+            mm([(R("pV", B, B), R("hsel", B * t, B, 1, p40), R("hq", 0, B, 1, p40)), (R("pV", B, B), R("Bb", 0, B), R("cmp", B * t, B))])
+            act(R("rr", B * t, B), R("pV", B, B), Fn.Relu, bias=bc, scale=sc)
+            tt(R("wb", wb + 4 * B, B), X(R("nxi", 0, A), aw), R("rr", B * t, B), Alu.min)
+            mm([(R("pV", 0, 8), R("Z", 15 - r, B), R("wb", wb + 4 * B + r, 8, 16)) for r in range(16)])
+            act(R("aout", 8 * t, 8), R("pV", 0, 8))
+            send(R("aout", 8 * t, 8), R("ain", 8 * (t + 1), 8), "r_a%d" % (t + 1))
+            tt(R("wb", wb, B), R("pN", po, B), ohk, Alu.mult)
+            tt(R("wb", wb + B, B), R("pN", po, B), ohj, Alu.mult)
+            tt(R("wb", wb + 2 * B, B), R("pN", qo, B), ohj, Alu.mult)
+            for c in range(8):
+                ts(R("eq1", 8 * B * t + B * c + 16 * c, B - 16 * c), R("arep", B * t + 16 * c, B - 16 * c),
+                   R("awb", 8 * t + c, 1), Alu.is_equal, R("wwb", c, 1), Alu.mult)
+            mm([(R("pW", 0, B), R("ones", 0, B, 1, p1), R("nthr", 0, B, 1, p1))]
+               + [(R("pW", 16 * c, B - 16 * c), R("Bb", 0, B), R("eq1", 8 * B * t + B * c + 16 * c, B - 16 * c)) for c in range(8)])
+            act(R("sg1", B * t, B), R("pW", 0, B), Fn.Sign)
+            mm([(R("pR", 0, 24), R("Z", 15 - r, B), R("wb", wb + r, 24, 16)) for r in range(16)]
+               + [(R("pR", 16, 8), R("Z2", 15 - r, B), R("sg1", B * t + r, 8, 16)) for r in range(16)])
+            nc, na, rest, qn, t2 = [R("sm", sm + 8 * i, 8) for i in range(5)]
+            act(na, R("pR", 16, 8), Fn.Sign, bias=-2000.0)
+            act(qn, R("pR", 16, 8), bias=D - 4096.0)
+            act(R("tl", tl + 16, 8), R("pR", 8, 8))
+            if t >= 2:
+                act(rest, R("pR", 8, 8), Fn.Relu, scale=8192.0, bias=4096.0 - 8192.0 * (n0 - B))
+            tt(nc, na, R("nw", 8 * (t // 2), 8), Alu.mult)
+            tt(R("tl", tl, 8), R("pR", 0, 8), nc, Alu.max)
+            tt(R("tl", tl + 8, 8), af, nc, Alu.max)
+            cp(R("lst", tl, 24), R("tl", tl, 24))
+            lpk, la, lpj = R("lst", tl, 8), R("lst", tl + 8, 8), R("lst", tl + 16, 8)
+            tt(X(R(Pn, 0, n0 + B), la), R("pq", pq + po, B), R("hn", B * t, B), Alu.max)
+            if t >= 2:
+                tt(qn, qn, rest, Alu.subtract)
+            mm([(R("pW", 2 * B, B), R("Bh", 0, B), R("wb", wb + 2 * B, B))])
+            act(R("qrep", B * t, B), R("pW", 2 * B, B), bias=D - 2048.0)
+            for c in range(8):
+                ts(R("eq2", 8 * B * t + B * c + 16 * c, B - 16 * c), R("qrep", B * t + 16 * c, B - 16 * c),
+                   R("sm", sm + 24 + c, 1), Alu.is_equal, R("ww", c, 1), Alu.mult)
+            mm([(R("pX", 0, B), R("ones", 0, B, 1, p1), R("nthr", 0, B, 1, p1))]
+               + [(R("pX", 16 * c, B - 16 * c), R("Bb", 0, B), R("eq2", 8 * B * t + B * c + 16 * c, B - 16 * c)) for c in range(8)])
+            act(R("sg", B * t, B), R("pX", 0, B), Fn.Sign)
+            mm([(R("pX", B, 8), R("id1", 0, B), qn)] + [(R("pX", B, 8), R("Z2", 15 - r, B), R("sg", B * t + r, 8, 16)) for r in range(16)])
+            tt(t2, R("pX", B, 8), R("iw", 0, 8), Alu.max)
+            cp(R("lt", 8 * t, 8), t2)
+        pb = 2048 * (t % 2)
+        wy, wx = (R("vb", 0, W0), R("ub", 0, W0)) if t == 0 else (R(Yn, D, lim[Yn]), R(Xn, D, lim[Xn]))
+        z, bg = R("zb", 0, B) if t == 0 else R("zin", B * t, B), R("bg", B * t, B)
+        n, last = NS[t], None
+        w = B // n
+        for h in range(n):
+            act(R("py", pb + 16 * w * h, 16 * w), X(wy, R("off", off + qo + w * h, w)))
+            ops[-1]["push"] = -30.0 * h
+        act(bg, X(R("base", 0, A), aw))
+        way = SUMS[t]
+        for h in range(4):
+            tt(R("prod", pb + 512 * h, 512), X(wx, R("off", off + po + 32 * h, 32)), R("py", pb + 512 * h, 512), Alu.mult)
+            ops[-1]["behind"], last = last, len(ops) - 1
+            if way[h] == "F":
+                mm([(R("pS", 64 * h, 64), R("idf", 0, B), R("prod", pb + 512 * h + k, 64, 8)) for k in range(8)])
+            elif way[h] == "H" and h % 2:
+                mm([(R("pS", 32 * (h - 1), 64), R("idf", 0, B), R("prod", pb + 512 * (h - 1) + k, 64, 16)) for k in range(16)])
+            elif way[h] == "S":
+                add("v", [("scan", R("run", 512 * (h % 2), 512), R("keep", 0, 512), R("prod", pb + 512 * h, 512), 0.0, Alu.add)], 512.0 * CY,
+                    [R("run", 512 * (h % 2), 512)], [R("keep", 0, 512), R("prod", pb + 512 * h, 512)])
+        m, zn, zo = 32 * (4 - way.count("S")), z[0], z[1]
+        if "S" in way:
+            act(R("z16", B * t + m, B - m), R(zn, zo + m, B - m), scale=1.0 / 16)
+            tt(R("pT", m, B - m), R("run", 512 * (m // 32 % 2) + 15, B - m, 16), R("z16", B * t + m, B - m), Alu.mult)
+        if "F" in way:
+            act(R("odd", 0, m), R("pS", 1, m, 2))
+            tt(R("pT", 3 * B, m), R("pS", 0, m, 2), R("odd", 0, m), Alu.add)
+            tt(R("pT", 0, m), R("pT", 3 * B, m), R(zn, zo, m), Alu.mult)
+        else:
+            tt(R("pT", 0, m), R("pS", 0, m), R(zn, zo, m), Alu.mult)
+        yo = R("yo", B * t, B)
+        if t == STEPS:
+            tt(yo, R("pT", 0, B), bg, Alu.add)
+        else:
+            if t in OPT_F:
+                e = R("pS", 3 * B, B)
+                tt(yo, R("pT", 0, B), bg, Alu.add)
+                mm([(e, R("idnb", 0, B), R("tgb", 0, B)), (e, R("idf", 0, B), yo)])
+                ts(R("zout", B * t, B), yo, 1.0, Alu.min, -1.0, Alu.max)
+            else:
+                e = R("pT", B, B)
+                tt(R("pY", 0, B), R("pT", 0, B), bg, Alu.add)
+                tt(e, R("pY", 0, B), R("tgb", 0, B), Alu.subtract)
+                ts(R("zout", B * t, B), R("pY", 0, B), 1.0, Alu.min, -1.0, Alu.max)
+                act(yo, R("pY", 0, B))
+            send(R("zout", B * t, B), R("zin", B * (t + 1), B), "r_z%d" % (t + 1))
+            u = R("cout", B * t, B)
+            act(u, X(R(Xn, D, n0 + B), lpk))
+            n1 = W0 + B * ((t + 1) // 2)
+            send(u, R("cfin", 0, B) if t == STEPS - 1 else R(Yn, D + n1, B), "r_c%d" % (t + 1))
+            act(R("wo", 2 * B * t, 2 * B), X(R("py", pb, 2048), R("lkj", 16 * t, 16)))
+            mm([(R("pY", 3 * B, B), R("idf", 0, B), u), (R("pY", 3 * B, B), R("idn", 0, B), R(Xn, D + n0, B))])
+            tt(R("more", B * t, B), R("pY", 3 * B, B), R("wo", 2 * B * t, B), Alu.mult)
+            tt(X(R("base", 0, n0 + B), la), bg, R("more", B * t, B), Alu.add)
+            if t in OPT_E:
+                act(R("xz", B * t, B), X(R(Xn, D, lim[Xn]), lpj), scale=1.0 if t in OPT_F else 1.0 / 16)
+                tt(R("pT", B, B), e, z, Alu.mult)
+                e = R("pT", B, B)
+            elif t in OPT_F:
+                tt(R("xz", B * t, B), X(R(Xn, D, lim[Xn]), lpj), z, Alu.mult)
+            else:
+                act(R("z16", B * t, B), z, scale=1.0 / 16)
+                tt(R("xz", B * t, B), X(R(Xn, D, lim[Xn]), lpj), R("z16", B * t, B), Alu.mult)
+            tt(R("less", B * t, B), e, R("xz", B * t, B), Alu.mult)
+            tt(X(R(Yn, 0, D + lim[Yn]), R("lt", 8 * t, 8)), R("wo", 2 * B * t + B, B), R("less", B * t, B), Alu.subtract)
+        dma("y", "d_out", [(In("ys", al, slice(B * t, B * t + B)), yo)], [], [yo], 100)
+        if t == STEPS - 1:
+            dma("y", "d_out", [(In("fb", al, al), R("base", 0, A))], [], [R("base", 0, A)], 200)
+            dma("y", "d_out", [(In("fc", al, al), R("cfin", 0, B))], [], [R("cfin", 0, B)], 100)
+    return ops
+
+
+def links(ops):
+    for j, o in enumerate(ops):
+        dep, soft = set(), [] if o.get("behind") is None else [o["behind"]]
+        o["soft"] = soft
+        if "after" in o:
+            dep.add(o["after"])
+        else:
+            for i in range(j):
+                p = ops[i]
+                if o.get("grp", -1) == p.get("grp", -2):
+                    continue
+                if o["eng"] == "t" and p["eng"] == "t" and o["wr"][0][0] == p["wr"][0][0]:
+                    soft.append(i)
+                for xs, ys, any_ in ((o["rd"], p["wr"], 0), (o["wr"], p["wr"], 0), (o["wr"], p["rd"], 0), (o["rd"], p["rd"], 1)):
+                    for a in xs:
+                        for b in ys:
+                            if a[0] == b[0]:
+                                if a[0] in PS and o["eng"] != p["eng"]:
+                                    dep.add(i)
+                                elif not any_ and a[1] < b[2] and b[1] < a[2]:
+                                    dep.add(i)
+        o["dep"] = dep
+
+
+def order(ops, rounds, seed=1):
+    n = len(ops)
+    eng, cost, lat = [o["eng"] for o in ops], [o["cost"] for o in ops], [o["lat"] for o in ops]
+    dep = [sorted(o["dep"]) for o in ops]
+    pre = [sorted(set(dep[j] + ops[j]["soft"])) for j in range(n)]
+    rank = [0.0] * n
+    users = [[] for j in range(n)]
+    for j in range(n - 1, -1, -1):
+        rank[j] += cost[j] + lat[j] + WAKE
+        for i in pre[j]:
+            rank[i] = max(rank[i], rank[j])
+            users[i].append(j)
+    rank = [rank[j] + ops[j].get("push", 0.0) for j in range(n)]
+
+    def lay(pr):
+        todo = [len(p) for p in pre]
+        done, at, free, seq = [0.0] * n, [0.0] * n, {None: 0.0}, []
+        for e in eng:
+            free[e] = 0.0
+        ready = {j: 0.0 for j in range(n) if todo[j] == 0}
+        while ready:
+            b, bk, bs = -1, 0, 0.0
+            for j, r in ready.items():
+                f = free[eng[j]]
+                st = r if r > f else f
+                k = int(st // SLACK)
+                if b < 0 or k < bk or (k == bk and pr[j] > pr[b]):
+                    b, bk, bs = j, k, st
+            if eng[b]:
+                free[eng[b]] = bs + cost[b]
+            at[b] = bs
+            done[b] = bs + cost[b] + lat[b]
+            del ready[b]
+            seq.append(b)
+            for k in users[b]:
+                todo[k] -= 1
+                if todo[k] == 0:
+                    ready[k] = max([done[i] + WAKE for i in dep[k]] + [0.0])
+        return max(done) + 0.02 * sum(done) / n, seq, at
+
+    best = lay(rank)
+    x, rank0 = seed, list(rank)
+    for it in range(rounds):
+        pr = list(rank)
+        for m in range(1 + it % 4):
+            x = (x * 1103515245 + 12345) % 2147483648
+            j = (x >> 8) % n
+            x = (x * 1103515245 + 12345) % 2147483648
+            dx = ((x >> 8) / 4194304.0 - 1.0) * JOG
+            todo = [j]
+            for lv in range(it % 7):
+                todo = todo + [i for k in todo for i in pre[k] if rank0[i] - rank0[j] < 2500.0]
+                todo = list(set(todo))
+            for k in todo:
+                pr[k] += dx
+        now = lay(pr)
+        if now[0] <= best[0]:
+            best, rank = now, pr
+    for j in range(n):
+        ops[j]["at"] = best[2][j]
+    return best[1]
+
+
+MEMO = {}
+
+
+def rank_program(g, core, T, topo):
+    rank = T.rank_of(core)
+    if rank is None:
+        return
+    if "ops" not in MEMO:
+        MEMO["ops"] = plan()
+        links(MEMO["ops"])
+        MEMO["seq"] = order(MEMO["ops"], ROUNDS)
+    ops, seq = MEMO["ops"], MEMO["seq"]
+    N = len(T.cores)
+    peers = [T.cores[(rank + 1) % N], T.cores[(rank - 1) % N]]
+    masks = []
+    for h, d in enumerate(peers):
+        e = topo.engines(core, d)
+        k = len(e) // 2
+        masks.append(sum(1 << x for x in e[h * k:h * k + k]))
+    lanes = sum(bin(m).count("1") for m in masks)
+    Q = {"v": g.vector, "s": g.scalar, "t": g.tensor, "g": g, "y": g.sync}
+
+    def ap(x):
+        if not isinstance(x, tuple):
+            return x
+        if x[0] == "*":
+            return ap(x[1]).indirect(ap(x[2]))
+        if x[0] == "@":
+            return T[x[1]][x[2]]
+        p = slice(None) if x[4] is None else x[4]
+        if x[3] == 1:
+            return T[x[0]][p, x[1]:x[1] + x[2]]
+        return T[x[0]][p, x[1]:x[1] + (x[2] - 1) * x[3] + 1:x[3]]
+
+    total, seen, mark = {}, {}, {}
+    for j in seq:
+        o = ops[j]
+        if o["eng"] is None:
+            mark[j] = (o["sem"][0], lanes)
+            total[o["sem"][0]] = lanes
+            continue
+        q = Q[o["eng"]]
+        need = {}
+        for i in o["dep"]:
+            if mark[i] is not None:
+                need[mark[i][0]] = max(need.get(mark[i][0], 0), mark[i][1])
+        for s, v in sorted(need.items()):
+            if seen.get((o["eng"], s), 0) < v:
+                q.wait_ge(T.sem[s], v)
+                seen[(o["eng"], s)] = v
+        s = "e_" + o["eng"]
+        for c in o["calls"]:
+            k, a = c[0], [ap(x) for x in c[1:]] if c[0] != "send" else None
+            if k == "send":
+                src, dst = c[1], c[2]
+                w = src[2] // 2
+                tr = []
+                for h, d in enumerate(peers):
+                    rid, pid = topo.addr(d, core)
+                    tr.append(RemoteDMATransfer(dst_ids=[DstId(rid=rid, pnc=pid)], dma_engine_mask=masks[h], remote_sem=T.sem[c[3]],
+                                                src=ap(R(src[0], src[1] + h * w, w)), dst=ap(R(dst[0], dst[1] + h * w, w))))
+                g.remote_dma_fused(tr, local_sem=T.sem.sent)
+                total["sent"] = total.get("sent", 0) + lanes
+                mark[j] = None
+                continue
+            if k == "dma":
+                s = c[3]
+                q.dma_start(a[0], a[1]).then_inc(T.sem[s], 16)
+                total[s] = total.get(s, 0) + 16
+                mark[j] = (s, total[s])
+                continue
+            if k == "tt":
+                r = q.tensor_tensor(a[0], a[1], a[2], a[3])
+            elif k == "ts":
+                r = q.tensor_scalar(a[0], a[1], a[2], None, a[4]) if a[5] is None else q.tensor_scalar(a[0], a[1], a[2], a[3], a[4], a[5])
+            elif k == "cp":
+                r = q.tensor_copy(a[0], a[1])
+            elif k == "ms":
+                r = q.memset(a[0], a[1])
+            elif k == "scan":
+                r = q.tensor_tensor_scan(a[0], a[1], a[2], a[3], Alu.mult, a[4])
+            elif k == "red":
+                r = q.tensor_reduce(a[0], a[1], AxisListType.X, Alu.add)
+            elif k == "act":
+                r = q.activation(a[0], a[1], a[2], bias=a[3], scale=a[4])
+            elif k == "sel":
+                r = q.affine_select(a[0], a[1], a[2], a[3], 0.0, 0, a[4])
+            elif k == "mm":
+                r = q.matmul(a[0], a[1], a[2], a[3], a[4])
+            elif SB[c[1][0]][1] == I32:
+                r = q.iota(a[0], a[1], 0, a[2])
+            else:
+                r = q.iota(a[0], a[1], 0, a[2], allow_small_or_imprecise_dtypes=True)
+            r.then_inc(T.sem[s], 1)
+            total[s] = total.get(s, 0) + 1
+            mark[j] = (s, total[s])
+    for s, v in sorted(total.items()):
+        g.sync.wait_ge(T.sem[s], v)

@@ -8,20 +8,20 @@ F, H, HF, I32, U16 = "float32", "bfloat16", "float16", "int32", "uint16"
 
 SB = {
     "U": (D + WIDE, F), "V": (D + W0 + 2 * B, F), "ub": (W0, H), "vb": (W0, H),
-    "uii": (A, I32), "voi": (A, I32), "NI": (WIDE, F), "NO": (WIDE, F), "base": (WIDE, F),
+    "uii": (A, I32), "voi": (A, I32), "NI": (WIDE + D, F), "NO": (WIDE + D, F), "base": (WIDE + D, F), "nn": (5 * B, F),
     "adi": (8, I32), "nxi": (A, I32), "hqi": (B, I32), "hq": (B, H), "lti": (B, I32), "ltb": (B, H),
     "zb": (B, H), "tgb": (B, H), "zin": (6 * B, F), "cfin": (B, F), "ain": (6 * 8, F),
     "J": (A, F), "gq": (B, F), "c80": (80, F), "pci": (8, I32), "col": (16, F), "id16": (16, F), "tmp16": (16, F),
     "idf": (B, F), "idb": (B, H), "Bb": (B, H), "Bh": (B, HF), "Z": (144, HF), "Z2": (144, H),
     "half": (B, F), "ones": (B, H), "thr": (B, F), "nthr": (B, H), "irow": (B, H),
-    "iw": (8, F), "ww": (8, F), "wwb": (8, H), "nw": (24, F), "kjf": (80, F), "kj": (80, U16), "lkj": (80, U16),
+    "iw": (8, F), "ww": (8, F), "wwb": (8, H), "nw": (72, F), "kjf": (80, F), "kj": (80, U16), "lkj": (80, U16),
     "aw": (6 * 8, U16), "awb": (5 * 8, H), "arep": (5 * B, H), "pq": (6 * 2 * B, F), "off": (6 * 2 * B, U16),
     "oh": (5 * 2 * B, H), "hn": (5 * B, F), "cmp": (5 * B, H), "rr": (5 * B, H),
     "wb": (5 * 5 * B, HF), "eq1": (5 * 8 * B, H), "eq2": (5 * 8 * B, H), "qrep": (5 * B, F), "sg": (5 * B, H),
     "aout": (5 * 8, F), "sm": (5 * 64, F), "tl": (5 * 24, F), "lst": (5 * 24, U16), "lt": (5 * 8, U16),
     "py": (2 * 2048, F), "prod": (2 * 2048, F), "bg": (6 * B, F), "z16": (6 * B, F), "yo": (6 * B, F),
     "zout": (5 * B, F), "cout": (5 * B, F), "wo": (10 * B, F), "wide1": (5 * B, H), "hsel": (5 * B, H), "pmx": (80, H), "xz": (5 * B, F),
-    "idn": (B, F), "odd": (B, F), "run": (1024, F), "keep": (512, H), "id1": (B, F), "idnb": (B, H), "sg1": (5 * B, H),
+    "idn": (B, F), "odd": (B, F), "w16": (5 * B, F), "run": (1024, F), "keep": (512, H), "id1": (B, F), "idnb": (B, H), "sg1": (5 * B, H),
     "less": (5 * B, F), "more": (5 * B, F),
 }
 PS = ["pS", "pN", "pW", "pR", "pV", "pT", "pY", "pX"]
@@ -31,10 +31,12 @@ DMAS = ["d_ad", "d_ui", "d_vo", "d_ub", "d_vb", "d_zt", "d_nx", "d_h", "d_lt", "
 SEMAPHORES = (["e_v", "e_s", "e_t", "e_g", "sent"] + DMAS
               + ["r_%s%d" % (k, t) for k in "azc" for t in range(1, STEPS + 1)])
 
-CY, PE, GATH, SCAT, HOP, WAKE = 1.0, 0.5, 1.6, 3.8, 2500.0, 120.0
-NS, SUMS = [4, 2, 2, 2, 2, 2], ["FFFF", "HHHH", "HHHH", "HHHH", "FFFF", "FFFS"]
-OPT_E, OPT_F, OPT_H = (), (0, 1, 2, 3), False
-ROUNDS, JOG, SLACK, PIECE = 12000, 5000.0, 20, 1000.0
+COSTS = [(0.83, 0.42, 1.56, 3.8, 3000.0), (0.87, 0.44, 1.1, 2.0, 3500.0), (1.15, 0.58, 2.0, 5.5, 2500.0)]
+WAKE = 180.0
+NS, SUMS = [4, 4, 4, 4, 4, 4], ["HHHH", "HHHH", "HHHH", "HHHH", "HHHH", "HHSS"]
+OPT_D, OPT_E, OPT_F, OPT_H = (0, 1, 2, 3, 4), (), (0, 1, 2, 3, 4), False
+OPT_W, SILU = [0, 0, 0, 0, 0], False
+ROUNDS, JOG, SLACK, PIECE, LEAD = 12000, 2000.0, 20, 1000.0, 3000.0
 
 
 def R(name, lo, n, step=1, p=None):
@@ -45,8 +47,9 @@ def X(win, off):
     return ("*", win, off)
 
 
-def plan():
+def plan(CY, PE, GATH, SCAT, HOP):
     ops = []
+    SH, MAGIC = (D, 1.5 * 2.0 ** 23) if SILU else (0, 0.0)
 
     def regs(x):
         if isinstance(x, tuple):
@@ -184,7 +187,9 @@ def plan():
     ts(R("ww", 0, 8), R("thr", 0, 8, 16), 1.0 / (6.25 * 2.0 ** 63), Alu.mult, vc, Alu.mult)
     act(R("wwb", 0, 8), R("ww", 0, 8))
     for m in range(3):
-        act(R("nw", 8 * m, 8), R("iw", 0, 8), scale=-1.0, bias=-float(W0 + B * m))
+        for ow, f in enumerate((-1.0, -1.0 / 2048, 1.0 / 16)):
+            if ow in OPT_W[2 * m:2 * m + 2]:
+                act(R("nw", 24 * ow + 8 * m, 8), R("iw", 0, 8), scale=f, bias=f * (W0 + B * m + SH))
     ts(R("hq", 0, B, 1, p40), R("hqi", 0, B, 1, p40), -2.0 if OPT_H else -1.0, Alu.mult)
     cp(R("ltb", 0, B, 1, p80), R("lti", 0, B, 1, p80))
     mm([(R("pR", 0, 80), R("ltb", 0, B, 1, p80), R("pmx", 0, 80, 1, p80))])
@@ -193,8 +198,10 @@ def plan():
     ts(R("lkj", 0, 80), R("kjf", 0, 80), r16, Alu.add)
     cp(R("aw", 0, 8), R("adi", 0, 8))
     cp(R("ain", 0, 8), R("adi", 0, 8))
-    cp(R("NO", 0, A), R("voi", 0, A))
-    cp(R("NI", 0, A), R("uii", 0, A))
+    ts(R("NO", 0, A), R("voi", 0, A), float(SH), Alu.add)
+    ts(R("NI", 0, A), R("uii", 0, A), float(SH), Alu.add)
+    if SILU:
+        ms(R("U", 0, D), 0.0); ms(R("V", 0, D), 0.0)
 
     for t in range(STEPS + 1):
         ev = t % 2 == 0
@@ -206,57 +213,87 @@ def plan():
         pq, off = 2 * B * t, 2 * B * t
         if t > 0:
             cp(aw, af)
-        act(R("pq", pq, B), X(R("NI", 0, A), aw))
-        act(R("pq", pq + B, B), X(R("NO", 0, A), aw))
-        cp(R("off", off + qo, B), R("pq", pq + qo, B))
-        cp(R("off", off + po, B), R("pq", pq + po, B))
+        act(R("pq", pq, B), X(R("NI", 0, A), aw), bias=MAGIC - SH)
+        act(R("pq", pq + B, B), X(R("NO", 0, A), aw), bias=MAGIC - SH)
+        ts(R("off", off + qo, B), R("pq", pq + qo, B), -MAGIC, Alu.add)
+        ts(R("off", off + po, B), R("pq", pq + po, B), -MAGIC, Alu.add)
         if t < STEPS:
             wb, sm, tl = 5 * B * t, 64 * t, 24 * t
             ohk, ohj = R("oh", 2 * B * t, B), R("oh", 2 * B * t + B, B)
-            act(R("pN", 0, 2 * B), R("pq", pq, 2 * B))
+            if SILU:
+                act(R("pN", 2 * B, B), R("pq", pq, B))
+            act(R("pN", 0, 2 * B), R("pq", pq, 2 * B), bias=SH - MAGIC)
             act(R("oh", 2 * B * t, 2 * B), X(R("id16", 0, 16), R("kj", 16 * t, 16)))
             act(R("arep", B * t, B), X(R("J", 0, A), aw), bias=-160.0)
             act(R("awb", 8 * t, 8), af, bias=-160.0)
             mm([(R("pR", B, B), R("idb", 0, B), ohk), (R("pR", B, B), R("ones", 0, B, 1, p1), R("irow", 0, B, 1, p1))])
-            act(R("hn", B * t, B), R("pR", B, B), scale=2048.0, bias=n0 - 2048.0)
+            act(R("hn", B * t, B), R("pR", B, B), scale=2048.0, bias=n0 + SH - 2048.0)
             if OPT_H:
                 mm([(R("pV", 2 * B, B), R("idf", 0, B), R("pq", pq, B)), (R("pV", 2 * B, B), R("idn", 0, B), R("pq", pq + B, B))])
                 act(R("cmp", B * t, B), R("pV", 2 * B, B), Fn.Sign, bias=-1.0 / 32)
             else:
-                tt(R("cmp", B * t, B), R("pN", 0, B), R("pq", pq + B, B), Alu.is_gt)
+                tt(R("cmp", B * t, B), R("pN", 2 * B if SILU else 0, B), R("pq", pq + B, B), Alu.is_gt)
             mm([(R("pV", B, B), R("hsel", B * t, B, 1, p40), R("hq", 0, B, 1, p40)), (R("pV", B, B), R("Bb", 0, B), R("cmp", B * t, B))])
             act(R("rr", B * t, B), R("pV", B, B), Fn.Relu, bias=bc, scale=sc)
-            tt(R("wb", wb + 4 * B, B), X(R("nxi", 0, A), aw), R("rr", B * t, B), Alu.min)
-            mm([(R("pV", 0, 8), R("Z", 15 - r, B), R("wb", wb + 4 * B + r, 8, 16)) for r in range(16)])
-            act(R("aout", 8 * t, 8), R("pV", 0, 8))
-            send(R("aout", 8 * t, 8), R("ain", 8 * (t + 1), 8), "r_a%d" % (t + 1))
+            ow = OPT_W[t]
+            tt(R("wb", wb + 3 * B, B), X(R("nxi", 0, A), aw), R("rr", B * t, B), Alu.min)
+            if ow == 0:
+                mm([(R("pV", 0, 8), R("Z", 15 - r, B), R("wb", wb + 3 * B + r, 8, 16)) for r in range(16)])
+                act(R("aout", 8 * t, 8), R("pV", 0, 8))
+                send(R("aout", 8 * t, 8), R("ain", 8 * (t + 1), 8), "r_a%d" % (t + 1))
             tt(R("wb", wb, B), R("pN", po, B), ohk, Alu.mult)
             tt(R("wb", wb + B, B), R("pN", po, B), ohj, Alu.mult)
             tt(R("wb", wb + 2 * B, B), R("pN", qo, B), ohj, Alu.mult)
+            if SILU:
+                tt(R("nn", B * t, B), R("pN", po, B), R("hn", B * t, B), Alu.max)
             for c in range(8):
                 ts(R("eq1", 8 * B * t + B * c + 16 * c, B - 16 * c), R("arep", B * t + 16 * c, B - 16 * c),
                    R("awb", 8 * t + c, 1), Alu.is_equal, R("wwb", c, 1), Alu.mult)
-            mm([(R("pW", 0, B), R("ones", 0, B, 1, p1), R("nthr", 0, B, 1, p1))]
-               + [(R("pW", 16 * c, B - 16 * c), R("Bb", 0, B), R("eq1", 8 * B * t + B * c + 16 * c, B - 16 * c)) for c in range(8)])
-            act(R("sg1", B * t, B), R("pW", 0, B), Fn.Sign)
-            mm([(R("pR", 0, 24), R("Z", 15 - r, B), R("wb", wb + r, 24, 16)) for r in range(16)]
-               + [(R("pR", 16, 8), R("Z2", 15 - r, B), R("sg1", B * t + r, 8, 16)) for r in range(16)])
+            w1 = [(R("pW", 16 * c, B - 16 * c), R("Bb", 0, B), R("eq1", 8 * B * t + B * c + 16 * c, B - 16 * c)) for c in range(8)]
             nc, na, rest, qn, t2 = [R("sm", sm + 8 * i, 8) for i in range(5)]
-            act(na, R("pR", 16, 8), Fn.Sign, bias=-2000.0)
-            act(qn, R("pR", 16, 8), bias=D - 4096.0)
+            if ow == 2:
+                mm(w1)
+                tt(R("wb", wb + 4 * B, B), R("pW", 0, B), R("thr", 0, B), Alu.is_gt)
+                mm([(R("pR", 0, 40), R("Z", 15 - r, B), R("wb", wb + r, 40, 16)) for r in range(16)])
+            else:
+                mm([(R("pW", 0, B), R("ones", 0, B, 1, p1), R("nthr", 0, B, 1, p1))] + w1)
+                act(R("sg1", B * t, B), R("pW", 0, B), Fn.Sign)
+            if ow == 0:
+                mm([(R("pR", 0, 24), R("Z", 15 - r, B), R("wb", wb + r, 24, 16)) for r in range(16)]
+                   + [(R("pR", 16, 8), R("Z2", 15 - r, B), R("sg1", B * t + r, 8, 16)) for r in range(16)])
+                act(na, R("pR", 16, 8), Fn.Sign, bias=-2000.0)
+                act(qn, R("pR", 16, 8), bias=D - SH - 4096.0)
+                tt(nc, na, R("nw", 8 * (t // 2), 8), Alu.mult)
+            else:
+                if ow == 1:
+                    mm([(R("pR", 0, 32), R("Z", 15 - r, B), R("wb", wb + r, 32, 16)) for r in range(16)])
+                act(R("aout", 8 * t, 8), R("pR", 24, 8))
+                send(R("aout", 8 * t, 8), R("ain", 8 * (t + 1), 8), "r_a%d" % (t + 1))
+                if ow == 1:
+                    mm([(R("pW", B, 8), R("Z2", 15 - r, B), R("sg1", B * t + r, 8, 16)) for r in range(16)])
+                    act(na, R("pW", B, 8), bias=D - SH - 4096.0)
+                    tt(nc, R("pW", B, 8), R("nw", 24 + 8 * (t // 2), 8), Alu.mult)
+                else:
+                    act(na, R("pR", 32, 8), scale=-256.0, bias=D - SH - 2048.0)
+                    tt(nc, R("pR", 32, 8), R("nw", 48 + 8 * (t // 2), 8), Alu.mult)
             act(R("tl", tl + 16, 8), R("pR", 8, 8))
             if t >= 2:
-                act(rest, R("pR", 8, 8), Fn.Relu, scale=8192.0, bias=4096.0 - 8192.0 * (n0 - B))
-            tt(nc, na, R("nw", 8 * (t // 2), 8), Alu.mult)
+                act(rest, R("pR", 8, 8), Fn.Relu, scale=8192.0, bias=4096.0 - 8192.0 * (n0 - B + SH))
+            if ow:
+                tt(qn, R("pR", 16, 8), na, Alu.add)
             tt(R("tl", tl, 8), R("pR", 0, 8), nc, Alu.max)
             tt(R("tl", tl + 8, 8), af, nc, Alu.max)
             cp(R("lst", tl, 24), R("tl", tl, 24))
             lpk, la, lpj = R("lst", tl, 8), R("lst", tl + 8, 8), R("lst", tl + 16, 8)
-            tt(X(R(Pn, 0, n0 + B), la), R("pq", pq + po, B), R("hn", B * t, B), Alu.max)
+            if SILU:
+                act(X(R(Pn, 0, n0 + B + SH), la), R("nn", B * t, B), Fn.Silu)
+                ops[-1]["cost"] = 65 + SCAT * B * CY + (1300.0 if t == 0 else 0.0)
+            else:
+                tt(X(R(Pn, 0, n0 + B), la), R("pq", pq + po, B), R("hn", B * t, B), Alu.max)
             if t >= 2:
                 tt(qn, qn, rest, Alu.subtract)
             mm([(R("pW", 2 * B, B), R("Bh", 0, B), R("wb", wb + 2 * B, B))])
-            act(R("qrep", B * t, B), R("pW", 2 * B, B), bias=D - 2048.0)
+            act(R("qrep", B * t, B), R("pW", 2 * B, B), bias=D - SH - 2048.0)
             for c in range(8):
                 ts(R("eq2", 8 * B * t + B * c + 16 * c, B - 16 * c), R("qrep", B * t + 16 * c, B - 16 * c),
                    R("sm", sm + 24 + c, 1), Alu.is_equal, R("ww", c, 1), Alu.mult)
@@ -313,22 +350,30 @@ def plan():
                 act(yo, R("pY", 0, B))
             send(R("zout", B * t, B), R("zin", B * (t + 1), B), "r_z%d" % (t + 1))
             u = R("cout", B * t, B)
-            act(u, X(R(Xn, D, n0 + B), lpk))
+            act(u, X(R(Xn, D - SH, n0 + B + SH), lpk))
             n1 = W0 + B * ((t + 1) // 2)
             send(u, R("cfin", 0, B) if t == STEPS - 1 else R(Yn, D + n1, B), "r_c%d" % (t + 1))
-            act(R("wo", 2 * B * t, 2 * B), X(R("py", pb, 2048), R("lkj", 16 * t, 16)))
-            mm([(R("pY", 3 * B, B), R("idf", 0, B), u), (R("pY", 3 * B, B), R("idn", 0, B), R(Xn, D + n0, B))])
-            tt(R("more", B * t, B), R("pY", 3 * B, B), R("wo", 2 * B * t, B), Alu.mult)
-            tt(X(R("base", 0, n0 + B), la), bg, R("more", B * t, B), Alu.add)
+            if t in OPT_D:
+                act(R("wo", 2 * B * t, 2 * B), X(R("py", pb, 2048), R("lkj", 16 * t, 16)))
+                mm([(R("pY", 3 * B, B), R("idf", 0, B), u), (R("pY", 3 * B, B), R("idn", 0, B), R(Xn, D + n0, B))])
+                tt(R("more", B * t, B), R("pY", 3 * B, B), R("wo", 2 * B * t, B), Alu.mult)
+            else:
+                act(R("wo", 2 * B * t, B), X(R("py", pb, 2048), R("lkj", 16 * t, 8)), scale=1.0 / 16)
+                act(R("wo", 2 * B * t + B, B), X(R("py", pb, 2048), R("lkj", 16 * t + 8, 8)))
+                act(R("pY", 3 * B, B), R(Xn, D + n0, B), scale=-1.0)
+                tt(R("pT", 2 * B, B), R("pY", 3 * B, B), u, Alu.add)
+                tt(R("more", B * t, B), R("pT", 2 * B, B), R("wo", 2 * B * t, B), Alu.mult)
+            tt(X(R("base", 0, n0 + B + SH), la), bg, R("more", B * t, B), Alu.add)
+            wj = X(R(Xn, D - SH, lim[Xn] + SH), lpj)
             if t in OPT_E:
-                act(R("xz", B * t, B), X(R(Xn, D, lim[Xn]), lpj), scale=1.0 if t in OPT_F else 1.0 / 16)
+                act(R("xz", B * t, B), wj, scale=1.0 if t in OPT_F else 1.0 / 16)
                 tt(R("pT", B, B), e, z, Alu.mult)
                 e = R("pT", B, B)
             elif t in OPT_F:
-                tt(R("xz", B * t, B), X(R(Xn, D, lim[Xn]), lpj), z, Alu.mult)
+                tt(R("xz", B * t, B), wj, z, Alu.mult)
             else:
                 act(R("z16", B * t, B), z, scale=1.0 / 16)
-                tt(R("xz", B * t, B), X(R(Xn, D, lim[Xn]), lpj), R("z16", B * t, B), Alu.mult)
+                tt(R("xz", B * t, B), wj, R("z16", B * t, B), Alu.mult)
             tt(R("less", B * t, B), e, R("xz", B * t, B), Alu.mult)
             tt(X(R(Yn, 0, D + lim[Yn]), R("lt", 8 * t, 8)), R("wo", 2 * B * t + B, B), R("less", B * t, B), Alu.subtract)
         dma("y", "d_out", [(In("ys", al, slice(B * t, B * t + B)), yo)], [], [yo], 100)
@@ -376,6 +421,9 @@ def order(ops, rounds, seed=1):
             users[i].append(j)
     rank = [rank[j] + ops[j].get("push", 0.0) for j in range(n)]
 
+    other = [([o["cost"] for o in p], [o["lat"] for o in p]) for p in [plan(*c) for c in COSTS]]
+    total = [50000.0, 50000.0, 70000.0]
+
     def lay(pr):
         todo = [len(p) for p in pre]
         done, at, free, seq = [0.0] * n, [0.0] * n, {None: 0.0}, []
@@ -400,10 +448,69 @@ def order(ops, rounds, seed=1):
                 todo[k] -= 1
                 if todo[k] == 0:
                     ready[k] = max([done[i] + WAKE for i in dep[k]] + [0.0])
-        return max(done) + 0.02 * sum(done) / n, seq, at
+        return value(seq, at, done, free)
 
+    def fit(pr):
+        todo = [len(p) for p in pre]
+        done, at, free, slots = [0.0] * n, [0.0] * n, {None: 0.0}, {}
+        for e in eng:
+            free[e], slots[e] = 0.0, []
+        ready = [j for j in range(n) if todo[j] == 0]
+        while ready:
+            b = max(ready, key=lambda j: pr[j])
+            ready.remove(b)
+            r, c = 0.0, cost[b]
+            for i in dep[b]:
+                if done[i] + WAKE > r:
+                    r = done[i] + WAKE
+            for i in soft[b]:
+                if at[i] + cost[i] > r:
+                    r = at[i] + cost[i]
+            if eng[b]:
+                s = slots[eng[b]]
+                k = len(s)
+                while k > 0 and s[k - 1][1] > r:
+                    k -= 1
+                while k < len(s) and s[k][0] < r + c:
+                    r = max(r, s[k][1])
+                    k += 1
+                s.insert(k, (r, r + c))
+            at[b], done[b] = r, r + c + lat[b]
+            for k in users[b]:
+                todo[k] -= 1
+                if todo[k] == 0:
+                    ready.append(k)
+        return value(sorted(range(n), key=lambda j: (at[j], j)), at, done, free)
+
+    def value(seq, at, done, free):
+        val = (max(done) + 0.02 * sum(done) / n) / total[0]
+        for m in range(1, len(other)):
+            cs, ls = other[m]
+            for e in free:
+                free[e] = 0.0
+            for j in seq:
+                st = free[eng[j]]
+                for i in dep[j]:
+                    if done[i] + WAKE > st:
+                        st = done[i] + WAKE
+                if eng[j]:
+                    free[eng[j]] = st + cs[j]
+                done[j] = st + cs[j] + ls[j]
+            val += max(done) / total[m]
+        return val, seq, at
+
+    soft = [o["soft"] for o in ops]
+    rank0 = list(rank)
+    if LEAD is not None:
+        lead = [o["calls"][:1] != [] and o["calls"][0][0] == "send" and o["calls"][0][1][0] == "aout" for o in ops]
+        for j in range(n - 1, -1, -1):
+            if lead[j]:
+                rank[j] += LEAD
+                for i in pre[j]:
+                    lead[i] = True
+        lay = fit
     best = lay(rank)
-    x, rank0 = seed, list(rank)
+    x = seed
     for it in range(rounds):
         pr = list(rank)
         for m in range(1 + it % 4):
@@ -433,7 +540,7 @@ def rank_program(g, core, T, topo):
     if rank is None:
         return
     if "ops" not in MEMO:
-        MEMO["ops"] = plan()
+        MEMO["ops"] = plan(*COSTS[0])
         links(MEMO["ops"])
         MEMO["seq"] = order(MEMO["ops"], ROUNDS)
     ops, seq = MEMO["ops"], MEMO["seq"]
@@ -508,6 +615,8 @@ def rank_program(g, core, T, topo):
                 r = q.tensor_tensor_scan(a[0], a[1], a[2], a[3], Alu.mult, a[4])
             elif k == "red":
                 r = q.tensor_reduce(a[0], a[1], AxisListType.X, Alu.add)
+            elif k == "act" and c[1][0] == "*":
+                r = q.activation(a[0], a[1], a[2])
             elif k == "act":
                 r = q.activation(a[0], a[1], a[2], bias=a[3], scale=a[4])
             elif k == "sel":

@@ -3,40 +3,44 @@ from concourse.mybir import AluOpType as Alu, ActivationFunctionType as Fn, Axis
 
 A, W0, B, STEPS = 320, 1536, 128, 5
 D = 128
-WIDE = W0 + 3 * B
+AW = D + W0 + 3 * B
 F, H, HF, I32, U16 = "float32", "bfloat16", "float16", "int32", "uint16"
+RHO, EDGE, BIG, HUGE = 1.7, 2.565, 32768.0, 1e17
 
 SB = {
-    "U": (D + WIDE, F), "V": (D + W0 + 2 * B, F), "ub": (W0, H), "vb": (W0, H),
-    "uii": (A, I32), "voi": (A, I32), "NI": (WIDE + D, F), "NO": (WIDE + D, F), "base": (WIDE + D, F), "nn": (5 * B, F),
-    "adi": (8, I32), "nxi": (A, I32), "hqi": (B, I32), "hq": (B, H), "lti": (B, I32), "ltb": (B, H),
-    "zb": (B, H), "tgb": (B, H), "zin": (6 * B, F), "cfin": (B, F), "ain": (6 * 8, F),
-    "J": (A, F), "gq": (B, F), "c80": (80, F), "pci": (8, I32), "col": (16, F), "id16": (16, F), "tmp16": (16, F),
-    "idf": (B, F), "idb": (B, H), "Bb": (B, H), "Bh": (B, HF), "Z": (144, HF), "Z2": (144, H),
-    "half": (B, F), "ones": (B, H), "thr": (B, F), "nthr": (B, H), "irow": (B, H),
-    "iw": (8, F), "ww": (8, F), "wwb": (8, H), "nw": (72, F), "kjf": (80, F), "kj": (80, U16), "lkj": (80, U16),
-    "aw": (6 * 8, U16), "awb": (5 * 8, H), "arep": (5 * B, H), "pq": (6 * 2 * B, F), "off": (6 * 2 * B, U16),
-    "oh": (5 * 2 * B, H), "hn": (5 * B, F), "cmp": (5 * B, H), "rr": (5 * B, H),
-    "wb": (5 * 5 * B, HF), "eq1": (5 * 8 * B, H), "eq2": (5 * 8 * B, H), "qrep": (5 * B, F), "sg": (5 * B, H),
-    "aout": (5 * 8, F), "sm": (5 * 64, F), "tl": (5 * 24, F), "lst": (5 * 24, U16), "lt": (5 * 8, U16),
+    "U": (D + W0 + 3 * B, F), "V": (D + W0 + 2 * B, F), "ub": (D + W0 + B, H), "vb": (D + W0, H),
+    "uii": (A, I32), "voi": (A, I32), "NI": (AW, F), "NO": (AW, F), "base": (AW, F), "nn": (5 * B, F),
+    "adi": (8, I32), "nxi": (A, I32), "wa": (5 * 3 * B, HF), "sa": (5 * 16, F), "xi": (2 * B, I32), "xq": (2 * B, H), "S": (5 * B, H),
+    "lti": (B, I32), "ltb": (B, H), "le": (B, HF), "re": (3 * B, HF), "lsq": (B, F), "val": (B, H), "Ja": (A, H), "c8": (24, F), "crow": (120, H), "Ci": (72, F),
+    "zb": (B, H), "tgb": (B, H), "zin": (6 * B, F), "cfin": (B, F),
+    "J": (B, F), "gq": (B, H), "lm": (B, H), "pci": (8, I32), "col": (16, F), "id16": (16, F), "tmp16": (16, F),
+    "idf": (B, F), "idn": (B, F), "id1": (B, F), "idh": (B, HF), "idhn": (B, HF), "idnb": (B, H),
+    "Bb": (B, H), "Z": (144, HF), "E16": (B, H), "N16": (B, H), "Rm": (32, H), "Cn": (72, F), "c160": (8, H),
+    "half": (B, F), "ones": (512, H), "wr": (B, F), "one": (8, F), "iw": (8, F), "wwb": (8, H), "ww": (8, F), "lkj": (120, U16),
+    "aw": (6 * 8, U16), "awb": (5 * 8, H), "arep": (5 * B, H), "pq": (6 * 2 * B, HF), "off": (6 * 2 * B, U16),
+    "wb": (5 * 3 * B, HF), "eq1": (2 * 8 * B, H), "eq2": (8 * B, H),
+    "f1": (5 * B, H), "f2": (5 * B, H), "qrep": (5 * B, HF), "sm": (5 * 16, F), "lst": (5 * 32, U16), "lt": (5 * 8, U16),
     "py": (2 * 2048, F), "prod": (2 * 2048, F), "bg": (6 * B, F), "z16": (6 * B, F), "yo": (6 * B, F),
-    "zout": (5 * B, F), "cout": (5 * B, F), "wo": (10 * B, F), "wide1": (5 * B, H), "hsel": (5 * B, H), "pmx": (80, H), "xz": (5 * B, F),
-    "idn": (B, F), "odd": (B, F), "w16": (5 * B, F), "run": (1024, F), "keep": (512, H), "id1": (B, F), "idnb": (B, H), "sg1": (5 * B, H),
-    "less": (5 * B, F), "more": (5 * B, F),
+    "zout": (5 * B, F), "cout": (5 * B, F), "wo": (10 * B, F), "pmx": (120, H), "xz": (5 * B, F), "dd": (5 * B, F),
+    "odd": (B, F), "run": (1024, F), "keep": (512, H), "less": (5 * B, F), "more": (5 * B, F),
 }
-PS = ["pS", "pN", "pW", "pR", "pV", "pT", "pY", "pX"]
+PS = ["pS", "pB", "pW", "pL", "pV", "pT", "pY", "pX"]
 SCRATCH = {k: ("sbuf", [128, v[0]], v[1]) for k, v in SB.items()}
 SCRATCH.update({k: ("psum", [128, 512], F) for k in PS})
-DMAS = ["d_ad", "d_ui", "d_vo", "d_ub", "d_vb", "d_zt", "d_nx", "d_h", "d_lt", "d_U", "d_V", "d_c", "d_b", "d_out"]
+DMAS = ["d_ad", "d_ui", "d_vo", "d_ub", "d_vb", "d_zt", "d_nx", "d_x", "d_lt", "d_lu", "d_U", "d_V", "d_c", "d_b", "d_out"]
 SEMAPHORES = (["e_v", "e_s", "e_t", "e_g", "sent"] + DMAS
               + ["r_%s%d" % (k, t) for k in "azc" for t in range(1, STEPS + 1)])
 
 COSTS = [(0.83, 0.42, 1.56, 3.8, 3000.0), (0.87, 0.44, 1.1, 2.0, 3500.0), (1.15, 0.58, 2.0, 5.5, 2500.0)]
 WAKE = 180.0
-NS, SUMS = [4, 4, 4, 4, 4, 4], ["HHHH", "HHHH", "HHHH", "HHHH", "HHHH", "HHSS"]
-OPT_D, OPT_E, OPT_F, OPT_H = (0, 1, 2, 3, 4), (), (0, 1, 2, 3, 4), False
-OPT_W, SILU = [0, 0, 0, 0, 0], False
-ROUNDS, JOG, SLACK, PIECE, LEAD = 12000, 2000.0, 20, 1000.0, 3000.0
+OPT = {"ns": [4, 4, 4, 4, 4, 4], "sums": ["HHHH", "FFFS", "FFFS", "FFFS", "FFFS", "HHSS"],
+       "cmp": "vvvvv",
+       "nx": "sssss",
+       "pick": "sssss", "thr1": "sssss", "thr2": "sssss", "name": "sssss", "qn": "sssss",
+       "d": "ttttt",
+       "xz": "vvvvv",
+       "qb": "pW"}
+ROUNDS, JOG, EASE, PIECE, TOTALS = 15000, 2000.0, 0.004, 1100.0, [45000.0, 45000.0, 65000.0]
 
 
 def R(name, lo, n, step=1, p=None):
@@ -49,7 +53,6 @@ def X(win, off):
 
 def plan(CY, PE, GATH, SCAT, HOP):
     ops = []
-    SH, MAGIC = (D, 1.5 * 2.0 ** 23) if SILU else (0, 0.0)
 
     def regs(x):
         if isinstance(x, tuple):
@@ -98,19 +101,20 @@ def plan(CY, PE, GATH, SCAT, HOP):
         add("v", [("cp", out, a)], vcost(out, [a], False), [out], [a])
 
     def ms(out, c):
-        add("v", [("ms", out, c)], max(64.0, size(out) * (0.5 if two(out) else 1.0)), [out], [])
+        add("v", [("ms", out, c)], max(64.0, size(out) * (0.5 if two(out) else 1.0)) * CY, [out], [])
 
-    def act(out, a, fn=Fn.Identity, bias=0.0, scale=1.0):
-        c = 65 + size(out) * CY * (GATH if a[0] == "*" else 1.0)
+    def act(out, a, fn=Fn.Identity, bias=0.0, scale=1.0, more=0.0):
+        c = 65 + more + size(out) * CY * (SCAT if out[0] == "*" else GATH if a[0] == "*" else 1.0)
         add("s", [("act", out, a, fn, bias, scale)], c, [out], [a, bias, scale])
 
     def mm(group):
         c, calls, part, last, gid = 0.0, [], [], None, len(ops)
-        for i, (o, l, r) in enumerate(group):
+        for i, m in enumerate(group):
+            o, l, r = m[:3]
             c += max(64, r[2]) * PE * (4 if SB[r[0]][1] == F else 1)
             calls.append(("mm", o, l, r, i == 0, i == len(group) - 1))
             part.append((o, l, r))
-            if c >= PIECE * PE or i == len(group) - 1:
+            if c >= PIECE * PE or i == len(group) - 1 or len(m) > 3:
                 j = add("t", calls, c, [x[0] for x in part], [x[1] for x in part] + [x[2] for x in part], lat=60.0)
                 ops[j]["grp"], ops[j]["behind"], last = gid, last, j
                 c, calls, part = 0.0, [], []
@@ -118,8 +122,11 @@ def plan(CY, PE, GATH, SCAT, HOP):
     def dma(eng, sem, pairs, outs, ins, ns):
         add(eng, [("dma", o, i, sem) for o, i in pairs], (900.0 if eng == "g" else 80.0) * len(pairs), outs, ins, lat=1800.0 + ns, sem=(sem, 16 * len(pairs)))
 
-    def iota(out, pat, cm=0):
-        add("g", [("iota", out, pat, cm)], 130 + 2 * size(out), [out], [])
+    def iota(out, pat, cm=0, base=0):
+        add("g", [("iota", out, pat, base, cm)], 130 + 2 * CY * size(out), [out], [])
+
+    def sel(out, a, pat, op, base, cm, fill=0.0):
+        add("g", [("sel", out, a, pat, op, fill, base, cm)], 170 + 2 * CY * size(out), [out], [a])
 
     def send(src, dst, sem):
         s = add("g", [("send", src, dst, sem)], 500.0, [], [src])
@@ -130,189 +137,184 @@ def plan(CY, PE, GATH, SCAT, HOP):
         return ("@", name, ix)
 
     al = slice(None)
+    p120, p80, p16, p2, p1 = slice(0, 120), slice(0, 80), slice(0, 16), slice(0, 2), slice(0, 1)
     dma("y", "d_ad", [(R("adi", 0, 8), In("ad", al, al))], [R("adi", 0, 8)], [], 0)
     dma("y", "d_vo", [(R("voi", 0, A), In("vo", al, al))], [R("voi", 0, A)], [], 100)
-    dma("s", "d_vb", [(R("vb", 0, W0), In("vt", al, al))], [R("vb", 0, W0)], [], 600)
+    dma("s", "d_vb", [(R("vb", D, W0), In("vt", al, al))], [R("vb", D, W0)], [], 600)
     dma("s", "d_ui", [(R("uii", 0, A), In("ui", al, al))], [R("uii", 0, A)], [], 300)
-    dma("y", "d_ub", [(R("ub", 0, W0), In("ut", al, al))], [R("ub", 0, W0)], [], 1000)
-    p80, p40, p1 = slice(0, 80), slice(0, 40), slice(0, 1)
+    dma("y", "d_ub", [(R("ub", D, W0), In("ut", al, al)), (R("ub", D + W0, B), In("cs", al, al))], [R("ub", D, W0 + B)], [], 1000)
     ms(R("nxi", 0, A), 0)
     dma("y", "d_nx", [(R("nxi", 0, A, 1, slice(q, 128, 16)), In("nx", al, slice(q * A, q * A + A))) for q in range(2)], [R("nxi", 0, A)], [], 300)
-    dma("y", "d_h", [(R("hqi", 0, B, 1, p40), In("hv", al, al))], [R("hqi", 0, B)], [], 100)
+    dma("s", "d_x", [(R("xi", B * q, B, 1, slice(h, 80, 2)), In(nm, al, al)) for h in range(2) for q, nm in enumerate(("sl", "tr"))], [R("xi", 0, 2 * B)], [], 100)
     dma("s", "d_zt", [(R("zb", 0, B), In("zs", al, al)), (R("tgb", 0, B), In("tg", al, al))], [R("zb", 0, B), R("tgb", 0, B)], [], 100)
-    dma("y", "d_lt", [(R("lti", 16 * g, 16, 1, slice(40 * q, 40 * q + 40)), In(nm, g, al)) for q, nm in enumerate(("sl", "tr")) for g in range(8)],
-        [R("lti", 0, B)], [], 100)
+    for e, sem, gs in (("y", "d_lt", range(0, 6)), ("s", "d_lu", range(6, 8))):
+        dma(e, sem, [(R("lti", 16 * g, 16, 1, slice(40 * q, 40 * q + 40)), In(nm, g, al)) for g in gs for q, nm in enumerate(("sl", "tr", "hv"))],
+            [R("lti", 16 * gs[0], 16 * len(gs))], [], 100)
+    pc, rc, gc_, par, r16, sc, vc, sT, l1, l2, sg = [R("col", i, 1) for i in range(11)]
+    sg80 = R("col", 10, 1, 1, p80)
     iota(R("pci", 0, 1), [[1, 1]], 1)
     iota(R("J", 0, B), [[1, B]])
     iota(R("gq", 0, B), [[1, 8], [0, 16]])
-    act(R("J", B, B), R("J", 0, B), bias=float(B))
-    act(R("J", 2 * B, A - 2 * B), R("J", 0, A - 2 * B), bias=2.0 * B)
-    iota(R("c80", 0, 80), [[0, 10], [256, 8]])
-    ms(R("wide1", 0, 5 * B), 1.0)
-    add("g", [("sel", R("hsel", 0, 5 * B, 1, p40), R("wide1", 0, 5 * B, 1, p40), [[1, 5], [5, 8], [0, 16]], Alu.is_equal, -1)], 170 + 10 * B, [R("hsel", 0, 5 * B)], [R("wide1", 0, 5 * B)])
-    add("g", [("sel", R("pmx", 0, 80, 1, p80), R("wide1", 0, 80, 1, p80), [[8, 5], [40, 2], [1, 8]], Alu.is_equal, -1)], 170 + 160, [R("pmx", 0, 80)], [R("wide1", 0, 80)])
-    if "S" in "".join(SUMS):
-        add("g", [("sel", R("keep", 0, 512), R("wide1", 0, 512), [[0, 32], [1, 16]], Alu.is_gt, 0)], 170 + 1024, [R("keep", 0, 512)], [R("wide1", 0, 512)])
+    iota(R("lm", 0, B), [[0, 8], [1024, 16]])
+    iota(R("Ja", 0, A), [[1, A]], 0, -160)
+    iota(R("c8", 0, 24), [[0, 3], [1, 8]])
+    iota(R("crow", 0, 120, 1, p1), [[0, 15], [256, 8]])
+    iota(R("Ci", 0, 72), [[B, 3], [0, 3], [16, 8]], 0, W0 + D)
+    for nm in ("vb", "ub", "U", "V"):
+        ms(R(nm, 0, D), 0.0)
+    ms(R("ones", 0, 512), 1.0)
+    ms(R("eq2", 0, 8 * B), 0.0)
+    ts(R("pci", 1, 1), R("pci", 0, 1), 15, Alu.bitwise_and)
+    ts(R("pci", 2, 1), R("pci", 0, 1), 4, Alu.arith_shift_right)
+    ts(R("pci", 3, 1), R("pci", 0, 1), 1, Alu.bitwise_and)
+    cp(R("col", 0, 4), R("pci", 0, 4))
+    act(R("Cn", 0, 72), R("Ci", 0, 72), Fn.Silu, bias=rc, more=1300.0)
+    ts(sg, par, -2.0, Alu.mult, 1.0, Alu.add)
+    ts(R("val", 0, B, 1, p80), R("lm", 0, B, 1, p80), sg80, Alu.mult, -1024.0, Alu.add)
+    for t in range(STEPS):
+        sel(R("S", B * t, B, 1, p80), R("val", 0, B, 1, p80), [[-10, 8], [0, 16]], Alu.is_ge, -2 * t, 1)
+        sel(R("S", B * t, B, 1, p80), R("S", B * t, B, 1, p80), [[10, 8], [0, 16]], Alu.is_ge, 2 * t + 1, -1)
+    for m in range(3):
+        iota(R("re", B * m, B, 1, p2), [[1, B]], 0, W0 + D + B * m)
+        sel(R("re", B * m, B, 1, p2), R("re", B * m, B, 1, p2), [[0, B]], Alu.is_gt, 0, 1, -2048.0)
+    act(R("lsq", 0, B, 1, p2), R("lm", 0, B, 1, p2), Fn.Square, scale=1.0 / 1024)
+    ts(R("lsq", 0, B, 1, p2), R("lsq", 0, B, 1, p2), -1.0, Alu.add)
+    sel(R("le", 0, B, 1, p2), R("lsq", 0, B, 1, p2), [[0, B]], Alu.is_equal, 0, 1, 1.0)
+    sel(R("pmx", 0, 120, 1, p120), R("ones", 0, 120, 1, p120), [[8, 5], [40, 3], [1, 8]], Alu.is_equal, 0, -1)
+    sel(R("E16", 0, B, 1, p16), R("ones", 0, B, 1, p16), [[0, 8], [1, 16]], Alu.is_equal, 0, -1)
+    sel(R("N16", 0, B, 1, p16), R("vb", 0, B, 1, p16), [[0, 8], [1, 16]], Alu.is_equal, 0, -1, -HUGE)
+    if "S" in "".join(OPT["sums"]):
+        sel(R("keep", 0, 512), R("ones", 0, 512), [[0, 32], [1, 16]], Alu.is_gt, 0, 0)
+    for nm, f in (("idf", 1.0 / 16), ("idnb", -1.0 / 16), ("idn", -1.0 / 16), ("id1", 1.0)):
+        sel(R(nm, 0, B), R("vb", 0, B), [[-1, B]], Alu.not_equal, 0, 1, f)
     dma("g", "d_b", [(R("base", 0, A), In("bs", al, al))], [R("base", 0, A)], [], 300)
     dma("g", "d_U", [(R("U", D, W0), In("ut", al, al))], [R("U", D, W0)], [], 1500)
     dma("g", "d_c", [(R("U", D + W0, B), In("cs", al, al))], [R("U", D + W0, B)], [], 200)
     dma("g", "d_V", [(R("V", D, W0), In("vt", al, al))], [R("V", D, W0)], [], 1500)
-    pc, rc, gc_, r16, sc, bc, vc = [R("col", i, 1) for i in range(7)]
-    ts(R("pci", 1, 1), R("pci", 0, 1), 15, Alu.bitwise_and)
-    ts(R("pci", 2, 1), R("pci", 0, 1), 4, Alu.arith_shift_right)
-    cp(R("col", 0, 3), R("pci", 0, 3))
-    ts(R("idf", 0, B), R("J", 0, B), pc, Alu.is_equal, 1.0 / 16, Alu.mult)
-    act(R("idn", 0, B), R("idf", 0, B), scale=-1.0)
-    act(R("id1", 0, B), R("idf", 0, B), scale=16.0)
-    act(R("idb", 0, B), R("idf", 0, B), scale=16.0)
-    if OPT_F:
-        act(R("idnb", 0, B), R("idf", 0, B), scale=-1.0)
+    ts(R("idh", 0, B), R("J", 0, B), pc, Alu.is_equal)
+    if "p" in OPT["cmp"]:
+        act(R("idhn", 0, B), R("idh", 0, B), scale=-1.0)
     ts(R("id16", 0, 16), R("J", 0, 16), rc, Alu.is_equal)
     ts(R("Bb", 0, B), R("gq", 0, B), gc_, Alu.is_equal)
-    ts(R("Bh", 0, B), R("gq", 0, B), gc_, Alu.is_equal)
-    ms(R("Z2", 0, 144), 0.0)
-    cp(R("Z", 0, 144), R("Z2", 0, 144))
-    ts(R("Z", 15, 8, 16), R("gq", 0, 8, 16), gc_, Alu.is_equal)
-    ts(R("Z2", 15, 8, 16), R("gq", 0, 8, 16), gc_, Alu.is_equal, -128.0, Alu.mult)
-    ms(R("half", 0, B), 0.5); ms(R("ones", 0, B), 1.0)
-    add("v", [("scan", R("thr", 0, B), R("half", 0, B), R("ones", 0, B), 2.5 * 2.0 ** 64, Alu.mult)], 128.0, [R("thr", 0, B)], [R("half", 0, B), R("ones", 0, B)])
-    act(R("nthr", 0, B), R("thr", 0, B), scale=-1.0)
-    act(R("irow", 0, B), R("J", 0, B), scale=1.0 / 2048)
+    ms(R("Z", 0, 144), 0.0)
+    ts(R("Z", 15, 8, 16), R("J", 0, 8), gc_, Alu.is_equal)
+    ts(R("Rm", 0, 24), R("c8", 0, 24), gc_, Alu.is_equal, BIG, Alu.mult)
+    act(R("Rm", 24, 8), R("Rm", 0, 8), scale=-1.0)
+    ms(R("c160", 0, 8), 160.0); ms(R("one", 0, 8), 1.0)
+    ms(R("half", 0, B), 1.0 / RHO)
+    add("v", [("scan", R("wr", 0, B), R("half", 0, B), R("ones", 0, B), RHO ** 64, Alu.mult)], B * CY, [R("wr", 0, B)], [R("half", 0, B), R("ones", 0, B)])
+    mm([(R("pX", 0, 1), R("wr", 0, B, 1, p1), R("one", 0, 1, 1, p1))])
+    add("v", [("rcp", sT, R("pX", 0, 1))], 200.0, [sT], [R("pX", 0, 1)])
     act(r16, rc, scale=16.0)
-    act(sc, R("id16", 0, 1), scale=-2048.0, bias=1024.0)
-    act(bc, sc, scale=17.0 if OPT_H else 0.5)
+    ts(l1, rc, rc, Alu.mult, -1.0, Alu.add)
+    act(l2, l1, scale=-2048.0)
+    act(sc, R("id16", 0, 1), scale=-2.0, bias=1.0)
     ts(R("iw", 0, 8), R("J", 0, 8, 16), rc, Alu.add)
-    tt(R("tmp16", 0, 16), R("thr", 0, 16), R("id16", 0, 16), Alu.mult)
-    add("v", [("red", vc, R("tmp16", 0, 16))], 64.0, [vc], [R("tmp16", 0, 16)])
-    ts(R("ww", 0, 8), R("thr", 0, 8, 16), 1.0 / (6.25 * 2.0 ** 63), Alu.mult, vc, Alu.mult)
-    act(R("wwb", 0, 8), R("ww", 0, 8))
-    for m in range(3):
-        for ow, f in enumerate((-1.0, -1.0 / 2048, 1.0 / 16)):
-            if ow in OPT_W[2 * m:2 * m + 2]:
-                act(R("nw", 24 * ow + 8 * m, 8), R("iw", 0, 8), scale=f, bias=f * (W0 + B * m + SH))
-    ts(R("hq", 0, B, 1, p40), R("hqi", 0, B, 1, p40), -2.0 if OPT_H else -1.0, Alu.mult)
-    cp(R("ltb", 0, B, 1, p80), R("lti", 0, B, 1, p80))
-    mm([(R("pR", 0, 80), R("ltb", 0, B, 1, p80), R("pmx", 0, 80, 1, p80))])
-    cp(R("kj", 0, 80), R("pR", 0, 80))
-    tt(R("kjf", 0, 80), R("pR", 0, 80), R("c80", 0, 80), Alu.add)
-    ts(R("lkj", 0, 80), R("kjf", 0, 80), r16, Alu.add)
+    tt(R("tmp16", 0, 16), R("wr", 0, 16), R("id16", 0, 16), Alu.mult)
+    add("v", [("red", vc, R("tmp16", 0, 16))], 64.0 * CY, [vc], [R("tmp16", 0, 16)])
+    for nm in ("wwb", "ww"):
+        ts(R(nm, 0, 8), R("wr", 0, 8, 16), RHO ** -63, Alu.mult, vc, Alu.mult)
+    act(R("xq", 0, 2 * B, 1, p80), R("xi", 0, 2 * B, 1, p80), Fn.Square, bias=sg80)
+    cp(R("ltb", 0, B, 1, p120), R("lti", 0, B, 1, p120))
+    mm([(R("pL", 0, 120), R("ones", 0, B, 1, p1), R("crow", 0, 120, 1, p1)), (R("pL", 0, 120), R("ltb", 0, B, 1, p120), R("pmx", 0, 120, 1, p120))])
+    ts(R("lkj", 0, 120), R("pL", 0, 120), r16, Alu.add)
     cp(R("aw", 0, 8), R("adi", 0, 8))
-    cp(R("ain", 0, 8), R("adi", 0, 8))
-    ts(R("NO", 0, A), R("voi", 0, A), float(SH), Alu.add)
-    ts(R("NI", 0, A), R("uii", 0, A), float(SH), Alu.add)
-    if SILU:
-        ms(R("U", 0, D), 0.0); ms(R("V", 0, D), 0.0)
+    act(R("NI", 0, A), R("uii", 0, A), bias=float(D))
+    act(R("NO", 0, A), R("voi", 0, A), bias=float(D))
+
+    def lowest(bank, eq, f, how):
+        mm([(R(bank, 0, B), R("E16", 0, B, 1, p16), R("N16", 0, B, 1, p16), "cut")]
+           + [(R(bank, 0, B), R(eq[0], eq[1] + B * c, B), R("Bb", 0, B)) + (("cut",) if c == 3 else ()) for c in range(8)])
+        if how == "s":
+            act(f, R(bank, 0, B), Fn.Relu, bias=-EDGE, scale=sT)
+        else:
+            ts(f, R(bank, 0, B), sT, Alu.mult, EDGE, Alu.is_gt)
 
     for t in range(STEPS + 1):
         ev = t % 2 == 0
         n0 = W0 + B * (t // 2)
-        lim = {"U": W0 + B * ((t + 1) // 2), "V": W0 + B * (t // 2)}
+        lim = {"U": D + W0 + B * ((t + 1) // 2), "V": D + W0 + B * (t // 2)}
         Xn, Yn, Pn = ("U", "V", "NI") if ev else ("V", "U", "NO")
         po, qo = (0, B) if ev else (B, 0)
-        aw, af = R("aw", 8 * t, 8), R("ain", 8 * t, 8)
-        pq, off = 2 * B * t, 2 * B * t
-        if t > 0:
-            cp(aw, af)
-        act(R("pq", pq, B), X(R("NI", 0, A), aw), bias=MAGIC - SH)
-        act(R("pq", pq + B, B), X(R("NO", 0, A), aw), bias=MAGIC - SH)
-        ts(R("off", off + qo, B), R("pq", pq + qo, B), -MAGIC, Alu.add)
-        ts(R("off", off + po, B), R("pq", pq + po, B), -MAGIC, Alu.add)
+        aw = R("aw", 8 * t, 8)
+        pq = off = 2 * B * t
+        P, Q = R("pq", pq + po, B), R("pq", pq + qo, B)
+        for o, nm, ni in ((B, "NO", "voi"), (0, "NI", "uii")):
+            if t == 0 or (t == 1 and nm == "NO"):
+                act(R("pq", pq + o, B), X(R(ni, 0, A), aw), bias=float(D))
+            else:
+                act(R("pq", pq + o, B), X(R(nm, 0, A), aw))
+            cp(R("off", off + o, B), R("pq", pq + o, B))
         if t < STEPS:
-            wb, sm, tl = 5 * B * t, 64 * t, 24 * t
-            ohk, ohj = R("oh", 2 * B * t, B), R("oh", 2 * B * t + B, B)
-            if SILU:
-                act(R("pN", 2 * B, B), R("pq", pq, B))
-            act(R("pN", 0, 2 * B), R("pq", pq, 2 * B), bias=SH - MAGIC)
-            act(R("oh", 2 * B * t, 2 * B), X(R("id16", 0, 16), R("kj", 16 * t, 16)))
-            act(R("arep", B * t, B), X(R("J", 0, A), aw), bias=-160.0)
-            act(R("awb", 8 * t, 8), af, bias=-160.0)
-            mm([(R("pR", B, B), R("idb", 0, B), ohk), (R("pR", B, B), R("ones", 0, B, 1, p1), R("irow", 0, B, 1, p1))])
-            act(R("hn", B * t, B), R("pR", B, B), scale=2048.0, bias=n0 + SH - 2048.0)
-            if OPT_H:
-                mm([(R("pV", 2 * B, B), R("idf", 0, B), R("pq", pq, B)), (R("pV", 2 * B, B), R("idn", 0, B), R("pq", pq + B, B))])
-                act(R("cmp", B * t, B), R("pV", 2 * B, B), Fn.Sign, bias=-1.0 / 32)
+            wa, wb, ls, m = 3 * B * t, 3 * B * t, 32 * t, t // 2
+            o = {k: v[t] for k, v in OPT.items() if len(v) == STEPS}
+            I_, O_, cm = R("pq", pq, B), R("pq", pq + B, B), R("wa", wa, B)
+            if o["cmp"] == "v":
+                tt(cm, I_, O_, Alu.is_le)
+            elif o["cmp"] == "g":
+                tt(cm, X(R("NI", 0, A), aw), O_, Alu.is_le)
             else:
-                tt(R("cmp", B * t, B), R("pN", 2 * B if SILU else 0, B), R("pq", pq + B, B), Alu.is_gt)
-            mm([(R("pV", B, B), R("hsel", B * t, B, 1, p40), R("hq", 0, B, 1, p40)), (R("pV", B, B), R("Bb", 0, B), R("cmp", B * t, B))])
-            act(R("rr", B * t, B), R("pV", B, B), Fn.Relu, bias=bc, scale=sc)
-            ow = OPT_W[t]
-            tt(R("wb", wb + 3 * B, B), X(R("nxi", 0, A), aw), R("rr", B * t, B), Alu.min)
-            if ow == 0:
-                mm([(R("pV", 0, 8), R("Z", 15 - r, B), R("wb", wb + 3 * B + r, 8, 16)) for r in range(16)])
-                act(R("aout", 8 * t, 8), R("pV", 0, 8))
-                send(R("aout", 8 * t, 8), R("ain", 8 * (t + 1), 8), "r_a%d" % (t + 1))
-            tt(R("wb", wb, B), R("pN", po, B), ohk, Alu.mult)
-            tt(R("wb", wb + B, B), R("pN", po, B), ohj, Alu.mult)
-            tt(R("wb", wb + 2 * B, B), R("pN", qo, B), ohj, Alu.mult)
-            if SILU:
-                tt(R("nn", B * t, B), R("pN", po, B), R("hn", B * t, B), Alu.max)
-            for c in range(8):
-                ts(R("eq1", 8 * B * t + B * c + 16 * c, B - 16 * c), R("arep", B * t + 16 * c, B - 16 * c),
-                   R("awb", 8 * t + c, 1), Alu.is_equal, R("wwb", c, 1), Alu.mult)
-            w1 = [(R("pW", 16 * c, B - 16 * c), R("Bb", 0, B), R("eq1", 8 * B * t + B * c + 16 * c, B - 16 * c)) for c in range(8)]
-            nc, na, rest, qn, t2 = [R("sm", sm + 8 * i, 8) for i in range(5)]
-            if ow == 2:
-                mm(w1)
-                tt(R("wb", wb + 4 * B, B), R("pW", 0, B), R("thr", 0, B), Alu.is_gt)
-                mm([(R("pR", 0, 40), R("Z", 15 - r, B), R("wb", wb + r, 40, 16)) for r in range(16)])
-            else:
-                mm([(R("pW", 0, B), R("ones", 0, B, 1, p1), R("nthr", 0, B, 1, p1))] + w1)
-                act(R("sg1", B * t, B), R("pW", 0, B), Fn.Sign)
-            if ow == 0:
-                mm([(R("pR", 0, 24), R("Z", 15 - r, B), R("wb", wb + r, 24, 16)) for r in range(16)]
-                   + [(R("pR", 16, 8), R("Z2", 15 - r, B), R("sg1", B * t + r, 8, 16)) for r in range(16)])
-                act(na, R("pR", 16, 8), Fn.Sign, bias=-2000.0)
-                act(qn, R("pR", 16, 8), bias=D - SH - 4096.0)
-                tt(nc, na, R("nw", 8 * (t // 2), 8), Alu.mult)
-            else:
-                if ow == 1:
-                    mm([(R("pR", 0, 32), R("Z", 15 - r, B), R("wb", wb + r, 32, 16)) for r in range(16)])
-                act(R("aout", 8 * t, 8), R("pR", 24, 8))
-                send(R("aout", 8 * t, 8), R("ain", 8 * (t + 1), 8), "r_a%d" % (t + 1))
-                if ow == 1:
-                    mm([(R("pW", B, 8), R("Z2", 15 - r, B), R("sg1", B * t + r, 8, 16)) for r in range(16)])
-                    act(na, R("pW", B, 8), bias=D - SH - 4096.0)
-                    tt(nc, R("pW", B, 8), R("nw", 24 + 8 * (t // 2), 8), Alu.mult)
+                mm([(R("pT", 2 * B, B), R("idh", 0, B), I_), (R("pT", 2 * B, B), R("idhn", 0, B), O_)])
+                ts(cm, R("pT", 2 * B, B), 0.5, Alu.is_lt)
+            for q, col in enumerate((R("id16", 0, 1), sc)):
+                if o["nx"][0] == "s" or q:
+                    act(R("wa", wa + B + B * q, B), X(R("nxi", 0, A), aw), scale=col)
                 else:
-                    act(na, R("pR", 32, 8), scale=-256.0, bias=D - SH - 2048.0)
-                    tt(nc, R("pR", 32, 8), R("nw", 48 + 8 * (t // 2), 8), Alu.mult)
-            act(R("tl", tl + 16, 8), R("pR", 8, 8))
-            if t >= 2:
-                act(rest, R("pR", 8, 8), Fn.Relu, scale=8192.0, bias=4096.0 - 8192.0 * (n0 - B + SH))
-            if ow:
-                tt(qn, R("pR", 16, 8), na, Alu.add)
-            tt(R("tl", tl, 8), R("pR", 0, 8), nc, Alu.max)
-            tt(R("tl", tl + 8, 8), af, nc, Alu.max)
-            cp(R("lst", tl, 24), R("tl", tl, 24))
-            lpk, la, lpj = R("lst", tl, 8), R("lst", tl + 8, 8), R("lst", tl + 16, 8)
-            if SILU:
-                act(X(R(Pn, 0, n0 + B + SH), la), R("nn", B * t, B), Fn.Silu)
-                ops[-1]["cost"] = 65 + SCAT * B * CY + (1300.0 if t == 0 else 0.0)
+                    ts(R("wa", wa + B + B * q, B), X(R("nxi", 0, A), aw), col, Alu.mult)
+            mm([(R("pV", 0, 24), R("Z", 15 - r, B), R("wa", wa + r, 24, 16)) for r in range(16)]
+               + [(R("pV", 0, 8), R("ltb", 0, B, 1, p120), R("pmx", 24 * t + 16, 8, 1, p120))])
+            ts(R("sa", 16 * t, 8), R("pV", 0, 8), 16.5, Alu.is_lt)
+            tt(R("sa", 16 * t + 8, 8), R("pV", 16, 8), R("sa", 16 * t, 8), Alu.mult)
+            tt(R("lst", ls + 24, 8), R("pV", 8, 8), R("sa", 16 * t + 8, 8), Alu.add)
+            send(R("lst", ls + 24, 8), R("aw", 8 * (t + 1), 8), "r_a%d" % (t + 1))
+            act(R("arep", B * t, B), X(R("Ja", 0, A), aw))
+            ts(R("awb", 8 * t, 8), aw, -160.0, Alu.add)
+            St = R("S", B * t, B, 1, p80)
+            mm([(R("pB", 0, 2 * B), St, R("xq", 0, 2 * B, 1, p80)), (R("pB", 2 * B, B), St, R("xq", B, B, 1, p80)),
+                (R("pB", 3 * B, B), St, R("xq", 0, B, 1, p80)), (R("pB", 3 * B, B), R("le", 0, B, 1, p2), R("re", B * m, B, 1, p2), "cut"),
+                (R("pB", 2 * B, B), R("idh", 0, B), Q), (R("pB", 0, B), R("idh", 0, B), P), (R("pB", B, B), R("idh", 0, B), P)])
+            if o["pick"] == "s":
+                act(R("wb", wb, 3 * B), R("pB", 0, 3 * B), Fn.Relu, bias=l2)
             else:
-                tt(X(R(Pn, 0, n0 + B), la), R("pq", pq + po, B), R("hn", B * t, B), Alu.max)
-            if t >= 2:
-                tt(qn, qn, rest, Alu.subtract)
-            mm([(R("pW", 2 * B, B), R("Bh", 0, B), R("wb", wb + 2 * B, B))])
-            act(R("qrep", B * t, B), R("pW", 2 * B, B), bias=D - SH - 2048.0)
+                ts(R("wb", wb, 3 * B), R("pB", 0, 3 * B), l2, Alu.add, 0.0, Alu.max)
+            tt(R("nn", B * t, B), R("pB", 3 * B, B), P, Alu.max)
+            e1 = 8 * B * (t % 2)
             for c in range(8):
-                ts(R("eq2", 8 * B * t + B * c + 16 * c, B - 16 * c), R("qrep", B * t + 16 * c, B - 16 * c),
-                   R("sm", sm + 24 + c, 1), Alu.is_equal, R("ww", c, 1), Alu.mult)
-            mm([(R("pX", 0, B), R("ones", 0, B, 1, p1), R("nthr", 0, B, 1, p1))]
-               + [(R("pX", 16 * c, B - 16 * c), R("Bb", 0, B), R("eq2", 8 * B * t + B * c + 16 * c, B - 16 * c)) for c in range(8)])
-            act(R("sg", B * t, B), R("pX", 0, B), Fn.Sign)
-            mm([(R("pX", B, 8), R("id1", 0, B), qn)] + [(R("pX", B, 8), R("Z2", 15 - r, B), R("sg", B * t + r, 8, 16)) for r in range(16)])
-            tt(t2, R("pX", B, 8), R("iw", 0, 8), Alu.max)
-            cp(R("lt", 8 * t, 8), t2)
+                ts(R("eq1", e1 + B * c, B), R("arep", B * t, B), R("awb", 8 * t + c, 1), Alu.is_equal, R("wwb", c, 1), Alu.mult)
+            lowest("pW", ("eq1", e1), R("f1", B * t, B), o["thr1"])
+            mm([(R("pL", 0, 8), R("idh", 0, B), R("awb", 8 * t, 8)), (R("pL", 0, 8), R("ones", 0, B, 1, p1), R("c160", 0, 8, 1, p1)),
+                ] + [(R("pL", 8, 24), R("Z", 15 - r, B), R("wb", wb + r, 24, 16)) + (("cut",) if r == 15 else ()) for r in range(16)]
+               + [(R("pL", 0, 24), R("f1", B * t, B), R("Rm", 0, 24))])
+            tt(R("lst", ls, 24), R("pL", 0, 24), R("Cn", 24 * m, 24), Alu.min)
+            la, lpk, lpj = R("lst", ls, 8), R("lst", ls + 8, 8), R("lst", ls + 16, 8)
+            rest, qn = R("sm", 16 * t, 8), R("sm", 16 * t + 8, 8)
+            edge = D + n0 - (B if t >= 2 else 0) - 0.5
+            if o["qn"] == "s":
+                act(rest, R("pL", 16, 8), Fn.Relu, scale=4096.0, bias=-4096.0 * edge)
+            else:
+                ts(rest, R("pL", 16, 8), edge, Alu.is_gt, 8192.0, Alu.mult)
+            tt(qn, R("pL", 24, 8), rest, Alu.subtract)
+            if o["name"] == "s":
+                act(X(R(Pn, 0, D + n0 + B), la), R("nn", B * t, B), Fn.Silu)
+            else:
+                cp(X(R(Pn, 0, D + n0 + B), la), R("nn", B * t, B))
+            qr = R(OPT["qb"], 2 * B, B)
+            mm([(qr, R("Bb", 0, B), R("wb", wb + 2 * B, B))])
+            for c in range(8):
+                ts(R("eq2", B * c + 16 * c, B - 16 * c), R(qr[0], qr[1] + 16 * c, B - 16 * c), R("sm", 16 * t + 8 + c, 1), Alu.is_equal, R("ww", c, 1), Alu.mult)
+            lowest("pX", ("eq2", 0), R("f2", B * t, B), o["thr2"])
+            mm([(R("pX", B, 8), R("id1", 0, B), qn, "cut"), (R("pX", B, 8), R("f2", B * t, B), R("Rm", 24, 8))])
+            tt(R("lt", 8 * t, 8), R("pX", B, 8), R("iw", 0, 8), Alu.max)
         pb = 2048 * (t % 2)
-        wy, wx = (R("vb", 0, W0), R("ub", 0, W0)) if t == 0 else (R(Yn, D, lim[Yn]), R(Xn, D, lim[Xn]))
+        wy, wx = (R("vb", 0, D + W0), R("ub", 0, D + W0)) if t == 0 else (R(Yn, 0, lim[Yn]), R(Xn, 0, lim[Xn]))
         z, bg = R("zb", 0, B) if t == 0 else R("zin", B * t, B), R("bg", B * t, B)
-        n, last = NS[t], None
+        n, last = OPT["ns"][t], None
         w = B // n
         for h in range(n):
             act(R("py", pb + 16 * w * h, 16 * w), X(wy, R("off", off + qo + w * h, w)))
             ops[-1]["push"] = -30.0 * h
         act(bg, X(R("base", 0, A), aw))
-        way = SUMS[t]
+        way = OPT["sums"][t]
         for h in range(4):
             tt(R("prod", pb + 512 * h, 512), X(wx, R("off", off + po + 32 * h, 32)), R("py", pb + 512 * h, 512), Alu.mult)
             ops[-1]["behind"], last = last, len(ops) - 1
@@ -323,59 +325,45 @@ def plan(CY, PE, GATH, SCAT, HOP):
             elif way[h] == "S":
                 add("v", [("scan", R("run", 512 * (h % 2), 512), R("keep", 0, 512), R("prod", pb + 512 * h, 512), 0.0, Alu.add)], 512.0 * CY,
                     [R("run", 512 * (h % 2), 512)], [R("keep", 0, 512), R("prod", pb + 512 * h, 512)])
-        m, zn, zo = 32 * (4 - way.count("S")), z[0], z[1]
+        k, zn, zo = 32 * (4 - way.count("S")), z[0], z[1]
         if "S" in way:
-            act(R("z16", B * t + m, B - m), R(zn, zo + m, B - m), scale=1.0 / 16)
-            tt(R("pT", m, B - m), R("run", 512 * (m // 32 % 2) + 15, B - m, 16), R("z16", B * t + m, B - m), Alu.mult)
+            act(R("z16", B * t + k, B - k), R(zn, zo + k, B - k), scale=1.0 / 16)
+            tt(R("pT", k, B - k), R("run", 512 * (k // 32 % 2) + 15, B - k, 16), R("z16", B * t + k, B - k), Alu.mult)
         if "F" in way:
-            act(R("odd", 0, m), R("pS", 1, m, 2))
-            tt(R("pT", 3 * B, m), R("pS", 0, m, 2), R("odd", 0, m), Alu.add)
-            tt(R("pT", 0, m), R("pT", 3 * B, m), R(zn, zo, m), Alu.mult)
+            act(R("odd", 0, k), R("pS", 1, k, 2))
+            tt(R("pT", 3 * B, k), R("pS", 0, k, 2), R("odd", 0, k), Alu.add)
+            tt(R("pT", 0, k), R("pT", 3 * B, k), R(zn, zo, k), Alu.mult)
         else:
-            tt(R("pT", 0, m), R("pS", 0, m), R(zn, zo, m), Alu.mult)
+            tt(R("pT", 0, k), R("pS", 0, k), R(zn, zo, k), Alu.mult)
         yo = R("yo", B * t, B)
-        if t == STEPS:
-            tt(yo, R("pT", 0, B), bg, Alu.add)
-        else:
-            if t in OPT_F:
-                e = R("pS", 3 * B, B)
-                tt(yo, R("pT", 0, B), bg, Alu.add)
-                mm([(e, R("idnb", 0, B), R("tgb", 0, B)), (e, R("idf", 0, B), yo)])
-                ts(R("zout", B * t, B), yo, 1.0, Alu.min, -1.0, Alu.max)
-            else:
-                e = R("pT", B, B)
-                tt(R("pY", 0, B), R("pT", 0, B), bg, Alu.add)
-                tt(e, R("pY", 0, B), R("tgb", 0, B), Alu.subtract)
-                ts(R("zout", B * t, B), R("pY", 0, B), 1.0, Alu.min, -1.0, Alu.max)
-                act(yo, R("pY", 0, B))
+        tt(yo, R("pT", 0, B), bg, Alu.add)
+        if t < STEPS:
+            e = R("pS", 3 * B, B)
+            mm([(e, R("idnb", 0, B), R("tgb", 0, B)), (e, R("idf", 0, B), yo)])
+            ts(R("zout", B * t, B), yo, 1.0, Alu.min, -1.0, Alu.max)
             send(R("zout", B * t, B), R("zin", B * (t + 1), B), "r_z%d" % (t + 1))
-            u = R("cout", B * t, B)
-            act(u, X(R(Xn, D - SH, n0 + B + SH), lpk))
+            u, c_, wall = R("cout", B * t, B), R(Xn, D + n0, B), R(Xn if t else "ub", 0, D + n0 + B)
+            act(u, X(wall, lpk))
             n1 = W0 + B * ((t + 1) // 2)
             send(u, R("cfin", 0, B) if t == STEPS - 1 else R(Yn, D + n1, B), "r_c%d" % (t + 1))
-            if t in OPT_D:
-                act(R("wo", 2 * B * t, 2 * B), X(R("py", pb, 2048), R("lkj", 16 * t, 16)))
-                mm([(R("pY", 3 * B, B), R("idf", 0, B), u), (R("pY", 3 * B, B), R("idn", 0, B), R(Xn, D + n0, B))])
-                tt(R("more", B * t, B), R("pY", 3 * B, B), R("wo", 2 * B * t, B), Alu.mult)
+            if o["d"] == "t":
+                act(R("wo", 2 * B * t, 2 * B), X(R("py", pb, 2048), R("lkj", 24 * t, 16)))
+                mm([(R("pY", 3 * B, B), R("idn", 0, B), c_, "cut"), (R("pY", 3 * B, B), R("idf", 0, B), u)])
             else:
-                act(R("wo", 2 * B * t, B), X(R("py", pb, 2048), R("lkj", 16 * t, 8)), scale=1.0 / 16)
-                act(R("wo", 2 * B * t + B, B), X(R("py", pb, 2048), R("lkj", 16 * t + 8, 8)))
-                act(R("pY", 3 * B, B), R(Xn, D + n0, B), scale=-1.0)
-                tt(R("pT", 2 * B, B), R("pY", 3 * B, B), u, Alu.add)
-                tt(R("more", B * t, B), R("pT", 2 * B, B), R("wo", 2 * B * t, B), Alu.mult)
-            tt(X(R("base", 0, n0 + B + SH), la), bg, R("more", B * t, B), Alu.add)
-            wj = X(R(Xn, D - SH, lim[Xn] + SH), lpj)
-            if t in OPT_E:
-                act(R("xz", B * t, B), wj, scale=1.0 if t in OPT_F else 1.0 / 16)
+                act(R("wo", 2 * B * t, B), X(R("py", pb, 2048), R("lkj", 24 * t, 8)), scale=1.0 / 16)
+                act(R("wo", 2 * B * t + B, B), X(R("py", pb, 2048), R("lkj", 24 * t + 8, 8)))
+                tt(R("pY", 3 * B, B), u, c_, Alu.subtract)
+            tt(R("more", B * t, B), R("pY", 3 * B, B), R("wo", 2 * B * t, B), Alu.mult)
+            tt(X(R("base", 0, D + n0 + B), la), bg, R("more", B * t, B), Alu.add)
+            wj = X(wall, lpj)
+            if o["xz"] == "s":
+                act(R("xz", B * t, B), wj)
                 tt(R("pT", B, B), e, z, Alu.mult)
                 e = R("pT", B, B)
-            elif t in OPT_F:
-                tt(R("xz", B * t, B), wj, z, Alu.mult)
             else:
-                act(R("z16", B * t, B), z, scale=1.0 / 16)
-                tt(R("xz", B * t, B), wj, R("z16", B * t, B), Alu.mult)
+                tt(R("xz", B * t, B), wj, z, Alu.mult)
             tt(R("less", B * t, B), e, R("xz", B * t, B), Alu.mult)
-            tt(X(R(Yn, 0, D + lim[Yn]), R("lt", 8 * t, 8)), R("wo", 2 * B * t + B, B), R("less", B * t, B), Alu.subtract)
+            tt(X(R(Yn, 0, lim[Yn]), R("lt", 8 * t, 8)), R("wo", 2 * B * t + B, B), R("less", B * t, B), Alu.subtract)
         dma("y", "d_out", [(In("ys", al, slice(B * t, B * t + B)), yo)], [], [yo], 100)
         if t == STEPS - 1:
             dma("y", "d_out", [(In("fb", al, al), R("base", 0, A))], [], [R("base", 0, A)], 200)
@@ -410,125 +398,94 @@ def links(ops):
 def order(ops, rounds, seed=1):
     n = len(ops)
     eng, cost, lat = [o["eng"] for o in ops], [o["cost"] for o in ops], [o["lat"] for o in ops]
-    dep = [sorted(o["dep"]) for o in ops]
-    pre = [sorted(set(dep[j] + ops[j]["soft"])) for j in range(n)]
-    rank = [0.0] * n
-    users = [[] for j in range(n)]
-    for j in range(n - 1, -1, -1):
-        rank[j] += cost[j] + lat[j] + WAKE
-        for i in pre[j]:
-            rank[i] = max(rank[i], rank[j])
-            users[i].append(j)
-    rank = [rank[j] + ops[j].get("push", 0.0) for j in range(n)]
+    near = []
+    for o in ops:
+        far = set()
+        for i in o["dep"]:
+            far.update(ops[i]["dep"])
+        near.append(sorted(o["dep"] - far))
+    fw = [[(i, cost[i] + lat[i] + WAKE) for i in near[j]] + [(i, cost[i]) for i in sorted(set(ops[j]["soft"][:1] + ops[j]["soft"][-1:]))] for j in range(n)]
+    bw = [[] for j in range(n)]
+    for j in range(n):
+        for i, d in fw[j]:
+            bw[i].append((j, cost[j] + d - cost[i]))
+    other = [([o["cost"] for o in p], [o["lat"] for o in p]) for p in [plan(*c) for c in COSTS[1:]]]
 
-    other = [([o["cost"] for o in p], [o["lat"] for o in p]) for p in [plan(*c) for c in COSTS]]
-    total = [50000.0, 50000.0, 70000.0]
-
-    def lay(pr):
+    def fit(key, pre, post, first):
         todo = [len(p) for p in pre]
-        done, at, free, seq = [0.0] * n, [0.0] * n, {None: 0.0}, []
-        for e in eng:
-            free[e] = 0.0
-        ready = {j: 0.0 for j in range(n) if todo[j] == 0}
+        at, slots = list(first), {e: [] for e in eng}
+        ready = sorted([(key[j], j) for j in range(n) if todo[j] == 0], reverse=True)
         while ready:
-            b, bk, bs = -1, 0, 0.0
-            for j, r in ready.items():
-                f = free[eng[j]]
-                st = r if r > f else f
-                k = int(st // SLACK)
-                if b < 0 or k < bk or (k == bk and pr[j] > pr[b]):
-                    b, bk, bs = j, k, st
-            if eng[b]:
-                free[eng[b]] = bs + cost[b]
-            at[b] = bs
-            done[b] = bs + cost[b] + lat[b]
-            del ready[b]
-            seq.append(b)
-            for k in users[b]:
-                todo[k] -= 1
-                if todo[k] == 0:
-                    ready[k] = max([done[i] + WAKE for i in dep[k]] + [0.0])
-        return value(seq, at, done, free)
-
-    def fit(pr):
-        todo = [len(p) for p in pre]
-        done, at, free, slots = [0.0] * n, [0.0] * n, {None: 0.0}, {}
-        for e in eng:
-            free[e], slots[e] = 0.0, []
-        ready = [j for j in range(n) if todo[j] == 0]
-        while ready:
-            b = max(ready, key=lambda j: pr[j])
-            ready.remove(b)
-            r, c = 0.0, cost[b]
-            for i in dep[b]:
-                if done[i] + WAKE > r:
-                    r = done[i] + WAKE
-            for i in soft[b]:
-                if at[i] + cost[i] > r:
-                    r = at[i] + cost[i]
+            b = ready.pop()[1]
+            r, c = at[b], cost[b]
+            for i, d in pre[b]:
+                if at[i] + d > r:
+                    r = at[i] + d
             if eng[b]:
                 s = slots[eng[b]]
                 k = len(s)
                 while k > 0 and s[k - 1][1] > r:
                     k -= 1
                 while k < len(s) and s[k][0] < r + c:
-                    r = max(r, s[k][1])
+                    if s[k][1] > r:
+                        r = s[k][1]
                     k += 1
                 s.insert(k, (r, r + c))
-            at[b], done[b] = r, r + c + lat[b]
-            for k in users[b]:
+            at[b] = r
+            more = False
+            for k, d in post[b]:
                 todo[k] -= 1
                 if todo[k] == 0:
-                    ready.append(k)
-        return value(sorted(range(n), key=lambda j: (at[j], j)), at, done, free)
+                    ready.append((key[k], k))
+                    more = True
+            if more:
+                ready.sort(reverse=True)
+        return at
 
-    def value(seq, at, done, free):
-        val = (max(done) + 0.02 * sum(done) / n) / total[0]
-        for m in range(1, len(other)):
-            cs, ls = other[m]
-            for e in free:
-                free[e] = 0.0
+    def value(at):
+        seq = sorted(range(n), key=lambda j: (at[j], j))
+        val = max(at[j] + cost[j] + lat[j] for j in range(n)) / TOTALS[0]
+        for m, (cs, ls) in enumerate(other):
+            free, done = {e: 0.0 for e in eng}, [0.0] * n
             for j in seq:
                 st = free[eng[j]]
-                for i in dep[j]:
+                for i in near[j]:
                     if done[i] + WAKE > st:
                         st = done[i] + WAKE
                 if eng[j]:
                     free[eng[j]] = st + cs[j]
                 done[j] = st + cs[j] + ls[j]
-            val += max(done) / total[m]
+            val += max(done) / TOTALS[m + 1]
         return val, seq, at
 
-    soft = [o["soft"] for o in ops]
-    rank0 = list(rank)
-    if LEAD is not None:
-        lead = [o["calls"][:1] != [] and o["calls"][0][0] == "send" and o["calls"][0][1][0] == "aout" for o in ops]
-        for j in range(n - 1, -1, -1):
-            if lead[j]:
-                rank[j] += LEAD
-                for i in pre[j]:
-                    lead[i] = True
-        lay = fit
-    best = lay(rank)
+    zero = [0.0] * n
+
+    def both(key):
+        back = fit([-key[j] - cost[j] for j in range(n)], bw, fw, lat)
+        return fit([-back[j] - cost[j] for j in range(n)], fw, bw, zero)
+
+    rank = [0.0] * n
+    for j in range(n - 1, -1, -1):
+        rank[j] = max([rank[k] + d - cost[k] + cost[j] for k, d in bw[j]] + [cost[j] + lat[j]])
+    best = now = value(fit([-r for r in rank], fw, bw, zero))
     x = seed
     for it in range(rounds):
-        pr = list(rank)
-        for m in range(1 + it % 4):
+        key = list(now[2])
+        for m in range(1 + it % 3):
             x = (x * 1103515245 + 12345) % 2147483648
             j = (x >> 8) % n
             x = (x * 1103515245 + 12345) % 2147483648
             dx = ((x >> 8) / 4194304.0 - 1.0) * JOG
             todo = [j]
-            for lv in range(it % 7):
-                todo = todo + [i for k in todo for i in pre[k] if rank0[i] - rank0[j] < 2500.0]
-                todo = list(set(todo))
+            for lv in range(it % 5):
+                todo = sorted(set(todo + [i for k in todo for i, d in fw[k] if key[j] - key[i] < 2500.0]))
             for k in todo:
-                pr[k] += dx
-        now = lay(pr)
-        if now[0] <= best[0]:
-            best, rank = now, pr
-    for j in range(n):
-        ops[j]["at"] = best[2][j]
+                key[k] += dx
+        new = value(both(key) if it % 4 == 0 else fit(key, fw, bw, zero))
+        if new[0] <= now[0] + EASE * (1.0 - it / rounds):
+            now = new
+            if new[0] < best[0]:
+                best = new
     return best[1]
 
 
@@ -615,18 +572,20 @@ def rank_program(g, core, T, topo):
                 r = q.tensor_tensor_scan(a[0], a[1], a[2], a[3], Alu.mult, a[4])
             elif k == "red":
                 r = q.tensor_reduce(a[0], a[1], AxisListType.X, Alu.add)
+            elif k == "rcp":
+                r = q.reciprocal(a[0], a[1])
             elif k == "act" and c[1][0] == "*":
                 r = q.activation(a[0], a[1], a[2])
             elif k == "act":
                 r = q.activation(a[0], a[1], a[2], bias=a[3], scale=a[4])
             elif k == "sel":
-                r = q.affine_select(a[0], a[1], a[2], a[3], 0.0, 0, a[4])
+                r = q.affine_select(a[0], a[1], a[2], a[3], a[4], a[5], a[6])
             elif k == "mm":
                 r = q.matmul(a[0], a[1], a[2], a[3], a[4])
             elif SB[c[1][0]][1] == I32:
-                r = q.iota(a[0], a[1], 0, a[2])
+                r = q.iota(a[0], a[1], a[2], a[3])
             else:
-                r = q.iota(a[0], a[1], 0, a[2], allow_small_or_imprecise_dtypes=True)
+                r = q.iota(a[0], a[1], a[2], a[3], allow_small_or_imprecise_dtypes=True)
             r.then_inc(T.sem[s], 1)
             total[s] = total.get(s, 0) + 1
             mark[j] = (s, total[s])

from concourse.bass import DstId, RemoteDMATransfer
from concourse.mybir import AluOpType as Alu, ActivationFunctionType as Fn, AxisListType

A, W0, B, STEPS = 320, 1536, 128, 5
D = 128
AW = D + W0 + 3 * B
F, H, HF, I32, U16 = "float32", "bfloat16", "float16", "int32", "uint16"
RHO, EDGE, BIG, HUGE = 1.7, 2.565, 32768.0, 1e17

SB = {
    "U": (D + W0 + 3 * B, F), "V": (D + W0 + 2 * B, F), "ub": (D + W0 + B, H), "vb": (D + W0, H),
    "uii": (A, I32), "voi": (A, I32), "NI": (AW, F), "NO": (AW, F), "base": (AW, F), "nn": (5 * B, F),
    "adi": (8, I32), "nxi": (A, I32), "wa": (5 * 3 * B, HF), "sa": (5 * 16, F), "xi": (2 * B, I32), "xq": (2 * B, H), "S": (5 * B, H),
    "lti": (B, I32), "ltb": (B, H), "le": (B, HF), "re": (3 * B, HF), "lsq": (B, F), "val": (B, H), "Ja": (A, H), "c8": (24, F), "crow": (120, H), "Ci": (72, F),
    "zb": (B, H), "tgb": (B, H), "zin": (6 * B, F), "cfin": (B, F),
    "J": (B, F), "gq": (B, H), "lm": (B, H), "pci": (8, I32), "col": (16, F), "id16": (16, F), "tmp16": (16, F),
    "idf": (B, F), "idn": (B, F), "id1": (B, F), "idh": (B, HF), "idhn": (B, HF), "idnb": (B, H),
    "Bb": (B, H), "Z": (144, HF), "E16": (B, H), "N16": (B, H), "Rm": (32, H), "Cn": (72, F), "c160": (8, H),
    "half": (B, F), "ones": (512, H), "wr": (B, F), "one": (8, F), "iw": (8, F), "wwb": (8, H), "ww": (8, F), "lkj": (120, U16),
    "aw": (6 * 8, U16), "awb": (5 * 8, H), "arep": (5 * B, H), "pq": (6 * 2 * B, HF), "off": (6 * 2 * B, U16),
    "wb": (5 * 3 * B, HF), "eq1": (2 * 8 * B, H), "eq2": (8 * B, H),
    "f1": (5 * B, H), "f2": (5 * B, H), "qrep": (5 * B, HF), "sm": (5 * 16, F), "lst": (5 * 32, U16), "lt": (5 * 8, U16),
    "py": (2 * 2048, F), "prod": (2 * 2048, F), "bg": (6 * B, F), "z16": (6 * B, F), "yo": (6 * B, F),
    "zout": (5 * B, F), "cout": (5 * B, F), "wo": (10 * B, F), "pmx": (120, H), "xz": (5 * B, F), "dd": (5 * B, F),
    "odd": (B, F), "run": (1024, F), "keep": (512, H), "less": (5 * B, F), "more": (5 * B, F),
}
PS = ["pS", "pB", "pW", "pL", "pV", "pT", "pY", "pX"]
SCRATCH = {k: ("sbuf", [128, v[0]], v[1]) for k, v in SB.items()}
SCRATCH.update({k: ("psum", [128, 512], F) for k in PS})
DMAS = ["d_ad", "d_ui", "d_vo", "d_ub", "d_vb", "d_zt", "d_nx", "d_x", "d_lt", "d_lu", "d_U", "d_V", "d_c", "d_b", "d_out"]
SEMAPHORES = (["e_v", "e_s", "e_t", "e_g", "sent"] + DMAS
              + ["r_%s%d" % (k, t) for k in "azc" for t in range(1, STEPS + 1)])

COSTS = [(0.83, 0.42, 1.56, 3.8, 3000.0), (0.87, 0.44, 1.1, 2.0, 3500.0), (1.15, 0.58, 2.0, 5.5, 2500.0)]
WAKE = 180.0
OPT = {"ns": [4, 4, 4, 4, 4, 4], "sums": ["HHHH", "FFFS", "FFFS", "FFFS", "FFFS", "HHSS"],
       "cmp": "vvvvv",
       "nx": "sssss",
       "pick": "sssss", "thr1": "sssss", "thr2": "sssss", "name": "sssss", "qn": "sssss",
       "d": "ttttt",
       "xz": "vvvvv",
       "qb": "pW"}
ROUNDS, JOG, EASE, PIECE, TOTALS = 15000, 2000.0, 0.004, 1100.0, [45000.0, 45000.0, 65000.0]


def R(name, lo, n, step=1, p=None):
    return (name, lo, n, step, p)


def X(win, off):
    return ("*", win, off)


def plan(CY, PE, GATH, SCAT, HOP):
    ops = []

    def regs(x):
        if isinstance(x, tuple):
            if x[0] == "*":
                return regs(x[1]) + regs(x[2])
            return [(x[0], x[1], x[1] + (x[2] - 1) * x[3] + 1)]
        return []

    def add(eng, calls, cost, outs, ins, lat=0.0, sem=None):
        rd, wr = [], []
        for o in outs:
            if o[0] == "*":
                wr += regs(o[1]); rd += regs(o[2])
            else:
                wr += regs(o)
        for i in ins:
            rd += regs(i)
        ops.append({"eng": eng, "calls": calls, "cost": cost, "rd": rd, "wr": wr, "lat": lat, "sem": sem})
        return len(ops) - 1

    def size(x):
        return 16 * x[2][2] if x[0] == "*" else x[2]

    def two(x):
        return x[0] in SB and SB[x[0]][1] in (H, HF, U16)

    def vcost(out, ins, both):
        n = size(out)
        if out[0] == "*":
            return 50 + SCAT * n * CY
        if ins[0][0] == "*":
            return 50 + GATH * n * CY
        if both:
            k = 1.0 if ins[0][0] in PS or ins[1][0] in PS else 2.0
        else:
            k = 0.5 if two(out) and all(two(i) for i in ins) else 1.0
        return max(64.0, k * n) * CY

    def tt(out, a, b, op):
        add("v", [("tt", out, a, b, op)], vcost(out, [a, b], True), [out], [a, b])

    def ts(out, a, s1, op0, s2=None, op1=None):
        add("v", [("ts", out, a, s1, s2, op0, op1)], vcost(out, [a], False), [out], [a, s1, s2])

    def cp(out, a):
        add("v", [("cp", out, a)], vcost(out, [a], False), [out], [a])

    def ms(out, c):
        add("v", [("ms", out, c)], max(64.0, size(out) * (0.5 if two(out) else 1.0)) * CY, [out], [])

    def act(out, a, fn=Fn.Identity, bias=0.0, scale=1.0, more=0.0):
        c = 65 + more + size(out) * CY * (SCAT if out[0] == "*" else GATH if a[0] == "*" else 1.0)
        add("s", [("act", out, a, fn, bias, scale)], c, [out], [a, bias, scale])

    def mm(group):
        c, calls, part, last, gid = 0.0, [], [], None, len(ops)
        for i, m in enumerate(group):
            o, l, r = m[:3]
            c += max(64, r[2]) * PE * (4 if SB[r[0]][1] == F else 1)
            calls.append(("mm", o, l, r, i == 0, i == len(group) - 1))
            part.append((o, l, r))
            if c >= PIECE * PE or i == len(group) - 1 or len(m) > 3:
                j = add("t", calls, c, [x[0] for x in part], [x[1] for x in part] + [x[2] for x in part], lat=60.0)
                ops[j]["grp"], ops[j]["behind"], last = gid, last, j
                c, calls, part = 0.0, [], []

    def dma(eng, sem, pairs, outs, ins, ns):
        add(eng, [("dma", o, i, sem) for o, i in pairs], (900.0 if eng == "g" else 80.0) * len(pairs), outs, ins, lat=1800.0 + ns, sem=(sem, 16 * len(pairs)))

    def iota(out, pat, cm=0, base=0):
        add("g", [("iota", out, pat, base, cm)], 130 + 2 * CY * size(out), [out], [])

    def sel(out, a, pat, op, base, cm, fill=0.0):
        add("g", [("sel", out, a, pat, op, fill, base, cm)], 170 + 2 * CY * size(out), [out], [a])

    def send(src, dst, sem):
        s = add("g", [("send", src, dst, sem)], 500.0, [], [src])
        r = add(None, [], 0.0, [dst], [], lat=HOP, sem=(sem, None))
        ops[r]["after"] = s

    def In(name, *ix):
        return ("@", name, ix)

    al = slice(None)
    p120, p80, p16, p2, p1 = slice(0, 120), slice(0, 80), slice(0, 16), slice(0, 2), slice(0, 1)
    dma("y", "d_ad", [(R("adi", 0, 8), In("ad", al, al))], [R("adi", 0, 8)], [], 0)
    dma("y", "d_vo", [(R("voi", 0, A), In("vo", al, al))], [R("voi", 0, A)], [], 100)
    dma("s", "d_vb", [(R("vb", D, W0), In("vt", al, al))], [R("vb", D, W0)], [], 600)
    dma("s", "d_ui", [(R("uii", 0, A), In("ui", al, al))], [R("uii", 0, A)], [], 300)
    dma("y", "d_ub", [(R("ub", D, W0), In("ut", al, al)), (R("ub", D + W0, B), In("cs", al, al))], [R("ub", D, W0 + B)], [], 1000)
    ms(R("nxi", 0, A), 0)
    dma("y", "d_nx", [(R("nxi", 0, A, 1, slice(q, 128, 16)), In("nx", al, slice(q * A, q * A + A))) for q in range(2)], [R("nxi", 0, A)], [], 300)
    dma("s", "d_x", [(R("xi", B * q, B, 1, slice(h, 80, 2)), In(nm, al, al)) for h in range(2) for q, nm in enumerate(("sl", "tr"))], [R("xi", 0, 2 * B)], [], 100)
    dma("s", "d_zt", [(R("zb", 0, B), In("zs", al, al)), (R("tgb", 0, B), In("tg", al, al))], [R("zb", 0, B), R("tgb", 0, B)], [], 100)
    for e, sem, gs in (("y", "d_lt", range(0, 6)), ("s", "d_lu", range(6, 8))):
        dma(e, sem, [(R("lti", 16 * g, 16, 1, slice(40 * q, 40 * q + 40)), In(nm, g, al)) for g in gs for q, nm in enumerate(("sl", "tr", "hv"))],
            [R("lti", 16 * gs[0], 16 * len(gs))], [], 100)
    pc, rc, gc_, par, r16, sc, vc, sT, l1, l2, sg = [R("col", i, 1) for i in range(11)]
    sg80 = R("col", 10, 1, 1, p80)
    iota(R("pci", 0, 1), [[1, 1]], 1)
    iota(R("J", 0, B), [[1, B]])
    iota(R("gq", 0, B), [[1, 8], [0, 16]])
    iota(R("lm", 0, B), [[0, 8], [1024, 16]])
    iota(R("Ja", 0, A), [[1, A]], 0, -160)
    iota(R("c8", 0, 24), [[0, 3], [1, 8]])
    iota(R("crow", 0, 120, 1, p1), [[0, 15], [256, 8]])
    iota(R("Ci", 0, 72), [[B, 3], [0, 3], [16, 8]], 0, W0 + D)
    for nm in ("vb", "ub", "U", "V"):
        ms(R(nm, 0, D), 0.0)
    ms(R("ones", 0, 512), 1.0)
    ms(R("eq2", 0, 8 * B), 0.0)
    ts(R("pci", 1, 1), R("pci", 0, 1), 15, Alu.bitwise_and)
    ts(R("pci", 2, 1), R("pci", 0, 1), 4, Alu.arith_shift_right)
    ts(R("pci", 3, 1), R("pci", 0, 1), 1, Alu.bitwise_and)
    cp(R("col", 0, 4), R("pci", 0, 4))
    act(R("Cn", 0, 72), R("Ci", 0, 72), Fn.Silu, bias=rc, more=1300.0)
    ts(sg, par, -2.0, Alu.mult, 1.0, Alu.add)
    ts(R("val", 0, B, 1, p80), R("lm", 0, B, 1, p80), sg80, Alu.mult, -1024.0, Alu.add)
    for t in range(STEPS):
        sel(R("S", B * t, B, 1, p80), R("val", 0, B, 1, p80), [[-10, 8], [0, 16]], Alu.is_ge, -2 * t, 1)
        sel(R("S", B * t, B, 1, p80), R("S", B * t, B, 1, p80), [[10, 8], [0, 16]], Alu.is_ge, 2 * t + 1, -1)
    for m in range(3):
        iota(R("re", B * m, B, 1, p2), [[1, B]], 0, W0 + D + B * m)
        sel(R("re", B * m, B, 1, p2), R("re", B * m, B, 1, p2), [[0, B]], Alu.is_gt, 0, 1, -2048.0)
    act(R("lsq", 0, B, 1, p2), R("lm", 0, B, 1, p2), Fn.Square, scale=1.0 / 1024)
    ts(R("lsq", 0, B, 1, p2), R("lsq", 0, B, 1, p2), -1.0, Alu.add)
    sel(R("le", 0, B, 1, p2), R("lsq", 0, B, 1, p2), [[0, B]], Alu.is_equal, 0, 1, 1.0)
    sel(R("pmx", 0, 120, 1, p120), R("ones", 0, 120, 1, p120), [[8, 5], [40, 3], [1, 8]], Alu.is_equal, 0, -1)
    sel(R("E16", 0, B, 1, p16), R("ones", 0, B, 1, p16), [[0, 8], [1, 16]], Alu.is_equal, 0, -1)
    sel(R("N16", 0, B, 1, p16), R("vb", 0, B, 1, p16), [[0, 8], [1, 16]], Alu.is_equal, 0, -1, -HUGE)
    if "S" in "".join(OPT["sums"]):
        sel(R("keep", 0, 512), R("ones", 0, 512), [[0, 32], [1, 16]], Alu.is_gt, 0, 0)
    for nm, f in (("idf", 1.0 / 16), ("idnb", -1.0 / 16), ("idn", -1.0 / 16), ("id1", 1.0)):
        sel(R(nm, 0, B), R("vb", 0, B), [[-1, B]], Alu.not_equal, 0, 1, f)
    dma("g", "d_b", [(R("base", 0, A), In("bs", al, al))], [R("base", 0, A)], [], 300)
    dma("g", "d_U", [(R("U", D, W0), In("ut", al, al))], [R("U", D, W0)], [], 1500)
    dma("g", "d_c", [(R("U", D + W0, B), In("cs", al, al))], [R("U", D + W0, B)], [], 200)
    dma("g", "d_V", [(R("V", D, W0), In("vt", al, al))], [R("V", D, W0)], [], 1500)
    ts(R("idh", 0, B), R("J", 0, B), pc, Alu.is_equal)
    if "p" in OPT["cmp"]:
        act(R("idhn", 0, B), R("idh", 0, B), scale=-1.0)
    ts(R("id16", 0, 16), R("J", 0, 16), rc, Alu.is_equal)
    ts(R("Bb", 0, B), R("gq", 0, B), gc_, Alu.is_equal)
    ms(R("Z", 0, 144), 0.0)
    ts(R("Z", 15, 8, 16), R("J", 0, 8), gc_, Alu.is_equal)
    ts(R("Rm", 0, 24), R("c8", 0, 24), gc_, Alu.is_equal, BIG, Alu.mult)
    act(R("Rm", 24, 8), R("Rm", 0, 8), scale=-1.0)
    ms(R("c160", 0, 8), 160.0); ms(R("one", 0, 8), 1.0)
    ms(R("half", 0, B), 1.0 / RHO)
    add("v", [("scan", R("wr", 0, B), R("half", 0, B), R("ones", 0, B), RHO ** 64, Alu.mult)], B * CY, [R("wr", 0, B)], [R("half", 0, B), R("ones", 0, B)])
    mm([(R("pX", 0, 1), R("wr", 0, B, 1, p1), R("one", 0, 1, 1, p1))])
    add("v", [("rcp", sT, R("pX", 0, 1))], 200.0, [sT], [R("pX", 0, 1)])
    act(r16, rc, scale=16.0)
    ts(l1, rc, rc, Alu.mult, -1.0, Alu.add)
    act(l2, l1, scale=-2048.0)
    act(sc, R("id16", 0, 1), scale=-2.0, bias=1.0)
    ts(R("iw", 0, 8), R("J", 0, 8, 16), rc, Alu.add)
    tt(R("tmp16", 0, 16), R("wr", 0, 16), R("id16", 0, 16), Alu.mult)
    add("v", [("red", vc, R("tmp16", 0, 16))], 64.0 * CY, [vc], [R("tmp16", 0, 16)])
    for nm in ("wwb", "ww"):
        ts(R(nm, 0, 8), R("wr", 0, 8, 16), RHO ** -63, Alu.mult, vc, Alu.mult)
    act(R("xq", 0, 2 * B, 1, p80), R("xi", 0, 2 * B, 1, p80), Fn.Square, bias=sg80)
    cp(R("ltb", 0, B, 1, p120), R("lti", 0, B, 1, p120))
    mm([(R("pL", 0, 120), R("ones", 0, B, 1, p1), R("crow", 0, 120, 1, p1)), (R("pL", 0, 120), R("ltb", 0, B, 1, p120), R("pmx", 0, 120, 1, p120))])
    ts(R("lkj", 0, 120), R("pL", 0, 120), r16, Alu.add)
    cp(R("aw", 0, 8), R("adi", 0, 8))
    act(R("NI", 0, A), R("uii", 0, A), bias=float(D))
    act(R("NO", 0, A), R("voi", 0, A), bias=float(D))

    def lowest(bank, eq, f, how):
        mm([(R(bank, 0, B), R("E16", 0, B, 1, p16), R("N16", 0, B, 1, p16), "cut")]
           + [(R(bank, 0, B), R(eq[0], eq[1] + B * c, B), R("Bb", 0, B)) + (("cut",) if c == 3 else ()) for c in range(8)])
        if how == "s":
            act(f, R(bank, 0, B), Fn.Relu, bias=-EDGE, scale=sT)
        else:
            ts(f, R(bank, 0, B), sT, Alu.mult, EDGE, Alu.is_gt)

    for t in range(STEPS + 1):
        ev = t % 2 == 0
        n0 = W0 + B * (t // 2)
        lim = {"U": D + W0 + B * ((t + 1) // 2), "V": D + W0 + B * (t // 2)}
        Xn, Yn, Pn = ("U", "V", "NI") if ev else ("V", "U", "NO")
        po, qo = (0, B) if ev else (B, 0)
        aw = R("aw", 8 * t, 8)
        pq = off = 2 * B * t
        P, Q = R("pq", pq + po, B), R("pq", pq + qo, B)
        for o, nm, ni in ((B, "NO", "voi"), (0, "NI", "uii")):
            if t == 0 or (t == 1 and nm == "NO"):
                act(R("pq", pq + o, B), X(R(ni, 0, A), aw), bias=float(D))
            else:
                act(R("pq", pq + o, B), X(R(nm, 0, A), aw))
            cp(R("off", off + o, B), R("pq", pq + o, B))
        if t < STEPS:
            wa, wb, ls, m = 3 * B * t, 3 * B * t, 32 * t, t // 2
            o = {k: v[t] for k, v in OPT.items() if len(v) == STEPS}
            I_, O_, cm = R("pq", pq, B), R("pq", pq + B, B), R("wa", wa, B)
            if o["cmp"] == "v":
                tt(cm, I_, O_, Alu.is_le)
            elif o["cmp"] == "g":
                tt(cm, X(R("NI", 0, A), aw), O_, Alu.is_le)
            else:
                mm([(R("pT", 2 * B, B), R("idh", 0, B), I_), (R("pT", 2 * B, B), R("idhn", 0, B), O_)])
                ts(cm, R("pT", 2 * B, B), 0.5, Alu.is_lt)
            for q, col in enumerate((R("id16", 0, 1), sc)):
                if o["nx"][0] == "s" or q:
                    act(R("wa", wa + B + B * q, B), X(R("nxi", 0, A), aw), scale=col)
                else:
                    ts(R("wa", wa + B + B * q, B), X(R("nxi", 0, A), aw), col, Alu.mult)
            mm([(R("pV", 0, 24), R("Z", 15 - r, B), R("wa", wa + r, 24, 16)) for r in range(16)]
               + [(R("pV", 0, 8), R("ltb", 0, B, 1, p120), R("pmx", 24 * t + 16, 8, 1, p120))])
            ts(R("sa", 16 * t, 8), R("pV", 0, 8), 16.5, Alu.is_lt)
            tt(R("sa", 16 * t + 8, 8), R("pV", 16, 8), R("sa", 16 * t, 8), Alu.mult)
            tt(R("lst", ls + 24, 8), R("pV", 8, 8), R("sa", 16 * t + 8, 8), Alu.add)
            send(R("lst", ls + 24, 8), R("aw", 8 * (t + 1), 8), "r_a%d" % (t + 1))
            act(R("arep", B * t, B), X(R("Ja", 0, A), aw))
            ts(R("awb", 8 * t, 8), aw, -160.0, Alu.add)
            St = R("S", B * t, B, 1, p80)
            mm([(R("pB", 0, 2 * B), St, R("xq", 0, 2 * B, 1, p80)), (R("pB", 2 * B, B), St, R("xq", B, B, 1, p80)),
                (R("pB", 3 * B, B), St, R("xq", 0, B, 1, p80)), (R("pB", 3 * B, B), R("le", 0, B, 1, p2), R("re", B * m, B, 1, p2), "cut"),
                (R("pB", 2 * B, B), R("idh", 0, B), Q), (R("pB", 0, B), R("idh", 0, B), P), (R("pB", B, B), R("idh", 0, B), P)])
            if o["pick"] == "s":
                act(R("wb", wb, 3 * B), R("pB", 0, 3 * B), Fn.Relu, bias=l2)
            else:
                ts(R("wb", wb, 3 * B), R("pB", 0, 3 * B), l2, Alu.add, 0.0, Alu.max)
            tt(R("nn", B * t, B), R("pB", 3 * B, B), P, Alu.max)
            e1 = 8 * B * (t % 2)
            for c in range(8):
                ts(R("eq1", e1 + B * c, B), R("arep", B * t, B), R("awb", 8 * t + c, 1), Alu.is_equal, R("wwb", c, 1), Alu.mult)
            lowest("pW", ("eq1", e1), R("f1", B * t, B), o["thr1"])
            mm([(R("pL", 0, 8), R("idh", 0, B), R("awb", 8 * t, 8)), (R("pL", 0, 8), R("ones", 0, B, 1, p1), R("c160", 0, 8, 1, p1)),
                ] + [(R("pL", 8, 24), R("Z", 15 - r, B), R("wb", wb + r, 24, 16)) + (("cut",) if r == 15 else ()) for r in range(16)]
               + [(R("pL", 0, 24), R("f1", B * t, B), R("Rm", 0, 24))])
            tt(R("lst", ls, 24), R("pL", 0, 24), R("Cn", 24 * m, 24), Alu.min)
            la, lpk, lpj = R("lst", ls, 8), R("lst", ls + 8, 8), R("lst", ls + 16, 8)
            rest, qn = R("sm", 16 * t, 8), R("sm", 16 * t + 8, 8)
            edge = D + n0 - (B if t >= 2 else 0) - 0.5
            if o["qn"] == "s":
                act(rest, R("pL", 16, 8), Fn.Relu, scale=4096.0, bias=-4096.0 * edge)
            else:
                ts(rest, R("pL", 16, 8), edge, Alu.is_gt, 8192.0, Alu.mult)
            tt(qn, R("pL", 24, 8), rest, Alu.subtract)
            if o["name"] == "s":
                act(X(R(Pn, 0, D + n0 + B), la), R("nn", B * t, B), Fn.Silu)
            else:
                cp(X(R(Pn, 0, D + n0 + B), la), R("nn", B * t, B))
            qr = R(OPT["qb"], 2 * B, B)
            mm([(qr, R("Bb", 0, B), R("wb", wb + 2 * B, B))])
            for c in range(8):
                ts(R("eq2", B * c + 16 * c, B - 16 * c), R(qr[0], qr[1] + 16 * c, B - 16 * c), R("sm", 16 * t + 8 + c, 1), Alu.is_equal, R("ww", c, 1), Alu.mult)
            lowest("pX", ("eq2", 0), R("f2", B * t, B), o["thr2"])
            mm([(R("pX", B, 8), R("id1", 0, B), qn, "cut"), (R("pX", B, 8), R("f2", B * t, B), R("Rm", 24, 8))])
            tt(R("lt", 8 * t, 8), R("pX", B, 8), R("iw", 0, 8), Alu.max)
        pb = 2048 * (t % 2)
        wy, wx = (R("vb", 0, D + W0), R("ub", 0, D + W0)) if t == 0 else (R(Yn, 0, lim[Yn]), R(Xn, 0, lim[Xn]))
        z, bg = R("zb", 0, B) if t == 0 else R("zin", B * t, B), R("bg", B * t, B)
        n, last = OPT["ns"][t], None
        w = B // n
        for h in range(n):
            act(R("py", pb + 16 * w * h, 16 * w), X(wy, R("off", off + qo + w * h, w)))
            ops[-1]["push"] = -30.0 * h
        act(bg, X(R("base", 0, A), aw))
        way = OPT["sums"][t]
        for h in range(4):
            tt(R("prod", pb + 512 * h, 512), X(wx, R("off", off + po + 32 * h, 32)), R("py", pb + 512 * h, 512), Alu.mult)
            ops[-1]["behind"], last = last, len(ops) - 1
            if way[h] == "F":
                mm([(R("pS", 64 * h, 64), R("idf", 0, B), R("prod", pb + 512 * h + k, 64, 8)) for k in range(8)])
            elif way[h] == "H" and h % 2:
                mm([(R("pS", 32 * (h - 1), 64), R("idf", 0, B), R("prod", pb + 512 * (h - 1) + k, 64, 16)) for k in range(16)])
            elif way[h] == "S":
                add("v", [("scan", R("run", 512 * (h % 2), 512), R("keep", 0, 512), R("prod", pb + 512 * h, 512), 0.0, Alu.add)], 512.0 * CY,
                    [R("run", 512 * (h % 2), 512)], [R("keep", 0, 512), R("prod", pb + 512 * h, 512)])
        k, zn, zo = 32 * (4 - way.count("S")), z[0], z[1]
        if "S" in way:
            act(R("z16", B * t + k, B - k), R(zn, zo + k, B - k), scale=1.0 / 16)
            tt(R("pT", k, B - k), R("run", 512 * (k // 32 % 2) + 15, B - k, 16), R("z16", B * t + k, B - k), Alu.mult)
        if "F" in way:
            act(R("odd", 0, k), R("pS", 1, k, 2))
            tt(R("pT", 3 * B, k), R("pS", 0, k, 2), R("odd", 0, k), Alu.add)
            tt(R("pT", 0, k), R("pT", 3 * B, k), R(zn, zo, k), Alu.mult)
        else:
            tt(R("pT", 0, k), R("pS", 0, k), R(zn, zo, k), Alu.mult)
        yo = R("yo", B * t, B)
        tt(yo, R("pT", 0, B), bg, Alu.add)
        if t < STEPS:
            e = R("pS", 3 * B, B)
            mm([(e, R("idnb", 0, B), R("tgb", 0, B)), (e, R("idf", 0, B), yo)])
            ts(R("zout", B * t, B), yo, 1.0, Alu.min, -1.0, Alu.max)
            send(R("zout", B * t, B), R("zin", B * (t + 1), B), "r_z%d" % (t + 1))
            u, c_, wall = R("cout", B * t, B), R(Xn, D + n0, B), R(Xn if t else "ub", 0, D + n0 + B)
            act(u, X(wall, lpk))
            n1 = W0 + B * ((t + 1) // 2)
            send(u, R("cfin", 0, B) if t == STEPS - 1 else R(Yn, D + n1, B), "r_c%d" % (t + 1))
            if o["d"] == "t":
                act(R("wo", 2 * B * t, 2 * B), X(R("py", pb, 2048), R("lkj", 24 * t, 16)))
                mm([(R("pY", 3 * B, B), R("idn", 0, B), c_, "cut"), (R("pY", 3 * B, B), R("idf", 0, B), u)])
            else:
                act(R("wo", 2 * B * t, B), X(R("py", pb, 2048), R("lkj", 24 * t, 8)), scale=1.0 / 16)
                act(R("wo", 2 * B * t + B, B), X(R("py", pb, 2048), R("lkj", 24 * t + 8, 8)))
                tt(R("pY", 3 * B, B), u, c_, Alu.subtract)
            tt(R("more", B * t, B), R("pY", 3 * B, B), R("wo", 2 * B * t, B), Alu.mult)
            tt(X(R("base", 0, D + n0 + B), la), bg, R("more", B * t, B), Alu.add)
            wj = X(wall, lpj)
            if o["xz"] == "s":
                act(R("xz", B * t, B), wj)
                tt(R("pT", B, B), e, z, Alu.mult)
                e = R("pT", B, B)
            else:
                tt(R("xz", B * t, B), wj, z, Alu.mult)
            tt(R("less", B * t, B), e, R("xz", B * t, B), Alu.mult)
            tt(X(R(Yn, 0, lim[Yn]), R("lt", 8 * t, 8)), R("wo", 2 * B * t + B, B), R("less", B * t, B), Alu.subtract)
        dma("y", "d_out", [(In("ys", al, slice(B * t, B * t + B)), yo)], [], [yo], 100)
        if t == STEPS - 1:
            dma("y", "d_out", [(In("fb", al, al), R("base", 0, A))], [], [R("base", 0, A)], 200)
            dma("y", "d_out", [(In("fc", al, al), R("cfin", 0, B))], [], [R("cfin", 0, B)], 100)
    return ops


def links(ops):
    for j, o in enumerate(ops):
        dep, soft = set(), [] if o.get("behind") is None else [o["behind"]]
        o["soft"] = soft
        if "after" in o:
            dep.add(o["after"])
        else:
            for i in range(j):
                p = ops[i]
                if o.get("grp", -1) == p.get("grp", -2):
                    continue
                if o["eng"] == "t" and p["eng"] == "t" and o["wr"][0][0] == p["wr"][0][0]:
                    soft.append(i)
                for xs, ys, any_ in ((o["rd"], p["wr"], 0), (o["wr"], p["wr"], 0), (o["wr"], p["rd"], 0), (o["rd"], p["rd"], 1)):
                    for a in xs:
                        for b in ys:
                            if a[0] == b[0]:
                                if a[0] in PS and o["eng"] != p["eng"]:
                                    dep.add(i)
                                elif not any_ and a[1] < b[2] and b[1] < a[2]:
                                    dep.add(i)
        o["dep"] = dep


def order(ops, rounds, seed=1):
    n = len(ops)
    eng, cost, lat = [o["eng"] for o in ops], [o["cost"] for o in ops], [o["lat"] for o in ops]
    near = []
    for o in ops:
        far = set()
        for i in o["dep"]:
            far.update(ops[i]["dep"])
        near.append(sorted(o["dep"] - far))
    fw = [[(i, cost[i] + lat[i] + WAKE) for i in near[j]] + [(i, cost[i]) for i in sorted(set(ops[j]["soft"][:1] + ops[j]["soft"][-1:]))] for j in range(n)]
    bw = [[] for j in range(n)]
    for j in range(n):
        for i, d in fw[j]:
            bw[i].append((j, cost[j] + d - cost[i]))
    other = [([o["cost"] for o in p], [o["lat"] for o in p]) for p in [plan(*c) for c in COSTS[1:]]]

    def fit(key, pre, post, first):
        todo = [len(p) for p in pre]
        at, slots = list(first), {e: [] for e in eng}
        ready = sorted([(key[j], j) for j in range(n) if todo[j] == 0], reverse=True)
        while ready:
            b = ready.pop()[1]
            r, c = at[b], cost[b]
            for i, d in pre[b]:
                if at[i] + d > r:
                    r = at[i] + d
            if eng[b]:
                s = slots[eng[b]]
                k = len(s)
                while k > 0 and s[k - 1][1] > r:
                    k -= 1
                while k < len(s) and s[k][0] < r + c:
                    if s[k][1] > r:
                        r = s[k][1]
                    k += 1
                s.insert(k, (r, r + c))
            at[b] = r
            more = False
            for k, d in post[b]:
                todo[k] -= 1
                if todo[k] == 0:
                    ready.append((key[k], k))
                    more = True
            if more:
                ready.sort(reverse=True)
        return at

    def value(at):
        seq = sorted(range(n), key=lambda j: (at[j], j))
        val = max(at[j] + cost[j] + lat[j] for j in range(n)) / TOTALS[0]
        for m, (cs, ls) in enumerate(other):
            free, done = {e: 0.0 for e in eng}, [0.0] * n
            for j in seq:
                st = free[eng[j]]
                for i in near[j]:
                    if done[i] + WAKE > st:
                        st = done[i] + WAKE
                if eng[j]:
                    free[eng[j]] = st + cs[j]
                done[j] = st + cs[j] + ls[j]
            val += max(done) / TOTALS[m + 1]
        return val, seq, at

    zero = [0.0] * n

    def both(key):
        back = fit([-key[j] - cost[j] for j in range(n)], bw, fw, lat)
        return fit([-back[j] - cost[j] for j in range(n)], fw, bw, zero)

    rank = [0.0] * n
    for j in range(n - 1, -1, -1):
        rank[j] = max([rank[k] + d - cost[k] + cost[j] for k, d in bw[j]] + [cost[j] + lat[j]])
    best = now = value(fit([-r for r in rank], fw, bw, zero))
    x = seed
    for it in range(rounds):
        key = list(now[2])
        for m in range(1 + it % 3):
            x = (x * 1103515245 + 12345) % 2147483648
            j = (x >> 8) % n
            x = (x * 1103515245 + 12345) % 2147483648
            dx = ((x >> 8) / 4194304.0 - 1.0) * JOG
            todo = [j]
            for lv in range(it % 5):
                todo = sorted(set(todo + [i for k in todo for i, d in fw[k] if key[j] - key[i] < 2500.0]))
            for k in todo:
                key[k] += dx
        new = value(both(key) if it % 4 == 0 else fit(key, fw, bw, zero))
        if new[0] <= now[0] + EASE * (1.0 - it / rounds):
            now = new
            if new[0] < best[0]:
                best = new
    return best[1]


MEMO = {}


def rank_program(g, core, T, topo):
    rank = T.rank_of(core)
    if rank is None:
        return
    if "ops" not in MEMO:
        MEMO["ops"] = plan(*COSTS[0])
        links(MEMO["ops"])
        MEMO["seq"] = order(MEMO["ops"], ROUNDS)
    ops, seq = MEMO["ops"], MEMO["seq"]
    N = len(T.cores)
    peers = [T.cores[(rank + 1) % N], T.cores[(rank - 1) % N]]
    masks = []
    for h, d in enumerate(peers):
        e = topo.engines(core, d)
        k = len(e) // 2
        masks.append(sum(1 << x for x in e[h * k:h * k + k]))
    lanes = sum(bin(m).count("1") for m in masks)
    Q = {"v": g.vector, "s": g.scalar, "t": g.tensor, "g": g, "y": g.sync}

    def ap(x):
        if not isinstance(x, tuple):
            return x
        if x[0] == "*":
            return ap(x[1]).indirect(ap(x[2]))
        if x[0] == "@":
            return T[x[1]][x[2]]
        p = slice(None) if x[4] is None else x[4]
        if x[3] == 1:
            return T[x[0]][p, x[1]:x[1] + x[2]]
        return T[x[0]][p, x[1]:x[1] + (x[2] - 1) * x[3] + 1:x[3]]

    total, seen, mark = {}, {}, {}
    for j in seq:
        o = ops[j]
        if o["eng"] is None:
            mark[j] = (o["sem"][0], lanes)
            total[o["sem"][0]] = lanes
            continue
        q = Q[o["eng"]]
        need = {}
        for i in o["dep"]:
            if mark[i] is not None:
                need[mark[i][0]] = max(need.get(mark[i][0], 0), mark[i][1])
        for s, v in sorted(need.items()):
            if seen.get((o["eng"], s), 0) < v:
                q.wait_ge(T.sem[s], v)
                seen[(o["eng"], s)] = v
        s = "e_" + o["eng"]
        for c in o["calls"]:
            k, a = c[0], [ap(x) for x in c[1:]] if c[0] != "send" else None
            if k == "send":
                src, dst = c[1], c[2]
                w = src[2] // 2
                tr = []
                for h, d in enumerate(peers):
                    rid, pid = topo.addr(d, core)
                    tr.append(RemoteDMATransfer(dst_ids=[DstId(rid=rid, pnc=pid)], dma_engine_mask=masks[h], remote_sem=T.sem[c[3]],
                                                src=ap(R(src[0], src[1] + h * w, w)), dst=ap(R(dst[0], dst[1] + h * w, w))))
                g.remote_dma_fused(tr, local_sem=T.sem.sent)
                total["sent"] = total.get("sent", 0) + lanes
                mark[j] = None
                continue
            if k == "dma":
                s = c[3]
                q.dma_start(a[0], a[1]).then_inc(T.sem[s], 16)
                total[s] = total.get(s, 0) + 16
                mark[j] = (s, total[s])
                continue
            if k == "tt":
                r = q.tensor_tensor(a[0], a[1], a[2], a[3])
            elif k == "ts":
                r = q.tensor_scalar(a[0], a[1], a[2], None, a[4]) if a[5] is None else q.tensor_scalar(a[0], a[1], a[2], a[3], a[4], a[5])
            elif k == "cp":
                r = q.tensor_copy(a[0], a[1])
            elif k == "ms":
                r = q.memset(a[0], a[1])
            elif k == "scan":
                r = q.tensor_tensor_scan(a[0], a[1], a[2], a[3], Alu.mult, a[4])
            elif k == "red":
                r = q.tensor_reduce(a[0], a[1], AxisListType.X, Alu.add)
            elif k == "rcp":
                r = q.reciprocal(a[0], a[1])
            elif k == "act" and c[1][0] == "*":
                r = q.activation(a[0], a[1], a[2])
            elif k == "act":
                r = q.activation(a[0], a[1], a[2], bias=a[3], scale=a[4])
            elif k == "sel":
                r = q.affine_select(a[0], a[1], a[2], a[3], a[4], a[5], a[6])
            elif k == "mm":
                r = q.matmul(a[0], a[1], a[2], a[3], a[4])
            elif SB[c[1][0]][1] == I32:
                r = q.iota(a[0], a[1], a[2], a[3])
            else:
                r = q.iota(a[0], a[1], a[2], a[3], allow_small_or_imprecise_dtypes=True)
            r.then_inc(T.sem[s], 1)
            total[s] = total.get(s, 0) + 1
            mark[j] = (s, total[s])
    for s, v in sorted(total.items()):
        g.sync.wait_ge(T.sem[s], v)
